import numpy as np, ml_dtypes
CORES = [51,54,179,182]
N = 4
BF = ml_dtypes.bfloat16
V, G, W, CAP, QA, QB, RO = 704, 672, 2048, 112, 4, 2, 4
def deal(rng, a):
    return np.stack([rng.permutation(np.resize(np.array(a), 8)) for q in range(N)])
def parts(rng):
    sh = (N, 8, 16, V)
    mid = rng.integers(20, 236, (N, 8, 16, 16)); kin = rng.integers(0, 16, (N, 8, 1, V))
    x = np.take_along_axis(mid, kin, 3) + rng.integers(-20, 21, sh)
    low = deal(rng, [0.003, 0.01, 0.03])[:, :, None, None]; flat = deal(rng, [0, 1])[:, :, None, None] == 1
    r = np.where(flat, 255, rng.integers(130, 256, sh)); r = np.where(rng.random(sh) < low, rng.integers(1, 130, sh), r)
    p = np.where(rng.random(sh) < 0.15, rng.integers(1, 130, sh), 0)
    keep = deal(rng, [0.4, 0.7, 0.9])[:, :, None, None]
    s = np.where(rng.random(sh) < keep, np.arange(V), rng.integers(0, W, sh))
    c = np.where(rng.random(sh) < 0.5, rng.integers(0, V, sh), rng.integers(0, W, sh))
    h = deal(rng, [180, 230, 500, 1000, 1200]) + rng.integers(0, 32, (N, 8))
    return x, r, p, c, s, h
def pack(x, r, p, c, s, h):
    v = {"x": x, "reach": r, "past": p}
    d = {k: np.ascontiguousarray(v[k].reshape(N, 128, V)).astype(np.float32).astype(BF) for k in v}
    d["cand"] = np.ascontiguousarray(c.reshape(N, 128, V)).astype(np.int32); d["succ"] = np.ascontiguousarray(s.reshape(N, 128, V)).astype(np.int32)
    d["th"] = h.reshape(N, 8, 1).astype(np.int32)
    return d
def setup_inputs(rng):
    return pack(*parts(rng))
def setup_inputs_ends(rng):
    sh = (N, 8, 16, V); one = (N, 8, 1, V)
    x = 255 * np.where(rng.random(one) < 0.7, rng.integers(0, 2, one), rng.integers(0, 2, sh))
    x = np.where((rng.random(one) < 0.2) & (rng.random(sh) < 0.3), x + np.where(x == 0, 1, -1), x)
    k = rng.random(one); r = np.where(k < 0.5, 255, np.where(k < 0.6, 1, np.where(rng.random(sh) < 0.5, 1, 255)))
    p = 255 * ((rng.random(one) < 0.25) & (rng.random(sh) < 0.2)).astype(np.int64)
    c = np.where(rng.random(sh) < 0.65, (W - 1) * rng.integers(0, 2, sh), rng.integers(0, W, sh))
    s = np.where((rng.random(one) < 0.5) | (rng.random(sh) < 0.65), (W - 1) * rng.integers(0, 2, sh), rng.integers(0, W, sh))
    h = 4095 * rng.integers(0, 2, (N, 8)); h[:, 0] = 0; h[:, 4] = 4095; h[:, 7] = 4095
    for a in (0, 1, V - QA, V - 1, G - 1): p[..., a] = 0; r[..., a] = 255
    p[..., 2] = 255; r[..., 2] = 1; x[..., 0] = 0; x[..., V - QA] = 0
    for a in (1, V - 1): x[:, 1::2, :, a] = 255; x[:, ::2, :, a] = 0
    c[..., 0] = 2; c[:, :, 15, 0] = V - 1
    c[..., V - QA] = 2; c[:, :, 14, V - QA] = V - 1; c[:, :, 15, V - QA] = 1
    s[..., 0] = 0; s[..., G - 1] = W - 1
    return pack(x, r, p, c, s, h)
def setup_inputs_corners(rng):
    x, r, p, c, s, h = parts(rng); act = np.arange(0, G, QB); here = np.arange(V); ptr = np.array([0, V - 1, V, V + G - 1, V + G, W - 1])
    for q in range(N):
        for g in range(8):
            k = (g + q) % 8
            if k < 6:
                n = (0, 1, CAP - 1, CAP, CAP + 1, len(act))[k]; a = rng.permutation(act)[:n]
                h[q, g] = 0; x[q, g] = x[q, g][:, rng.integers(0, 16, V)]; r[q, g] = 200; r[q, g, :, V - 1] = 5
                p[q, g] = np.where(rng.random((16, V)) < 0.05, 10, 0)
                w = np.tile(here, (16, 1)); w[rng.integers(0, 16, n), a] = V - 1; s[q, g] = w
            elif k == 6:
                h[q, g] = 4095; p[q, g] = 0; c[q, g] = here - here % QA + (here + QA - 1) % QA
            else:
                h[q, g] = 4095; full = rng.random(V) < 0.5; full[0] = True; full[V - 1] = False; m = rng.random(V) < 0.5; n = int(np.count_nonzero(m))
                w = p[q, g].copy(); w[:, full] = 255; p[q, g] = w
                w = np.where(rng.random((16, V)) < 0.5, rng.integers(V, W, (16, V)), (here + QA * rng.integers(0, V // QA, (16, V))) % V)
                w[:, m] = rng.choice(here[full], (16, n)); w[15, m] = rng.integers(0, V, n); c[q, g] = w
                s[q, g] = np.where(rng.random((16, V)) < 0.3, here, ptr[rng.integers(0, 6, (16, V))])
    return pack(x, r, p, c, s, h)
def setup_inputs_ties(rng):
    x, r, p, c, s, h = parts(rng); sh = (N, 8, 16, V)
    x = 8 * rng.integers(0, 2, sh); pool = rng.integers(0, V, (N, 8, 1, 24)); pool[..., 0] = 0; pool[..., 1] = V - 1; pool[..., 2] = V; pool[..., 3] = W - 1
    few = np.take_along_axis(pool, rng.integers(0, 24, sh), 3); c[:, ::2] = few[:, ::2]
    m = np.arange(16)[:, None] == rng.integers(0, 16, (N, 8, 1, 1))
    r = np.where(m, rng.integers(100, 102, sh), rng.integers(101, 256, sh)); p = np.where(m, rng.integers(99, 101, sh), 0)
    h = deal(rng, [24, 32, 40, 48, 64])
    return pack(x, r, p, c, s, h)
def setup_inputs_border(rng):
    x, r, p, c, s, h = parts(rng); x = rng.integers(0, 256, x.shape); h = rng.integers(1, 33, h.shape); s[...] = np.arange(V)
    goal = np.zeros((N, 8, 3), np.int64); e, y, w = G - 1, V - 3, V - 2
    for q in range(N):
        for g in range(8):
            n, turn = ((0, 0), (0, int(rng.integers(1, 3))), (CAP - 1, 0), (CAP, 0), (CAP + 1, 0), (G, 0))[(g + q) % 6]
            o = [4 * rng.permutation(G // 4 - 1) + i for i in range(4)]
            v = o[turn][0]; j = o[0][1]; v1 = o[1][1]; u = o[1][2]; b = o[3][1]; z = o[3][2]
            for a in (v, e, j, y, v1, w, u, b): s[q, g, :, a] = z; c[q, g, :, a] = rng.integers(V, W, 16)
            for a in (v, v1, u): r[q, g, :, a] = rng.integers(140, 200, 16); p[q, g, :, a] = rng.integers(0, 41, 16)
            for a in (e, j): r[q, g, :, a] = rng.integers(200, 255, 16); p[q, g, :, a] = 0
            for a in (y, w): r[q, g, :, a] = 255; p[q, g, :, a] = 0
            r[q, g, :, z] = 255; r[q, g, :, V - 1] = 1
            i, k = rng.integers(0, 16, 2); d = int(rng.integers(1, 41))
            r[q, g, :, b] = r[q, g, :, u]; p[q, g, :, b] = p[q, g, :, u]; r[q, g, i, b] -= d; p[q, g, k, b] += d
            for a, f in ((v, e), (j, y), (v1, y), (w, y), (u, b)): x[q, g, :, a] = x[q, g, :, f]
            for a, f in ((v, e), (j, y), (v1, j), (w, y), (u, b)): c[q, g, int(rng.integers(0, 16)), a] = f
            a = rng.permutation(np.setdiff1d(np.arange(0, G, QB), np.array([v, j])))[:n]
            s[q, g][rng.integers(0, 16, len(a)), a] = V - 1
            goal[q, g] = (e, u, j)
    k = np.arange(G, V - 3)
    for q in range(N):
        for g in range(8):
            see = np.concatenate([V + goal[(q + 1) % N, g], V + G + goal[(q - 1) % N, g]])
            r[q, g, :, G:V - 3] = 255; p[q, g, :, G:V - 3] = 0
            s[q, g][rng.integers(0, 16, len(k)), k] = see[((k - G) // 4) % 6]
    return pack(x, r, p, c, s, h)
def setup_inputs_spread(rng):
    sh = (N, 8, 16, V); one = (N, 8, 1, V)
    def uneven(): return np.floor(np.exp2(8 * rng.random(one)) * rng.random(sh)).astype(np.int64)
    def lean():
        e = deal(rng, [1.0, 2.0, 4.0])[:, :, None, None]; v = np.minimum((W * rng.random(sh) ** e).astype(np.int64), W - 1)
        return np.where(deal(rng, [0, 0, 1])[:, :, None, None] == 1, W - 1 - v, v)
    x = uneven(); r = np.maximum(255 - uneven(), 1); p = np.where(rng.random(one) < 0.3, uneven(), 0)
    c = lean(); s = np.where(rng.random(one) < rng.random(sh), np.arange(V), lean())
    h = np.minimum(np.floor(np.exp2(12 * rng.random((N, 8)))).astype(np.int64), 4095)
    return pack(x, r, p, c, s, h)
def check_inputs(d):
    bad = []
    for k, lo, hi in (("x", 0, 255), ("reach", 1, 255), ("past", 0, 255), ("cand", 0, W - 1), ("succ", 0, W - 1), ("th", 0, 4095)):
        a = np.asarray(d[k]).astype(np.float64)
        if not (np.all(a >= lo) and np.all(a <= hi)): bad.append("range of " + k)
        elif not np.all(a == np.floor(a)): bad.append("whole numbers in " + k)
    return bad
def at(a, ix):
    return np.take_along_axis(a, ix[:, :, None, :], 3)
def reference(x, reach, past, cand, succ, th):
    X = x.astype(np.float32).astype(np.int32).reshape(N, 8, 16, V)
    R = reach.astype(np.float32).astype(np.int32).reshape(N, 8, 16, V); P = past.astype(np.float32).astype(np.int32).reshape(N, 8, 16, V)
    R = np.concatenate([R, np.roll(R[..., :G], -1, axis=0), np.roll(R[..., :G], 1, axis=0)], axis=3)
    P = np.concatenate([P, np.roll(P[..., :G], -1, axis=0), np.roll(P[..., :G], 1, axis=0)], axis=3)
    C = cand.astype(np.int64).reshape(N, 8, 16, V); S = succ.astype(np.int64).reshape(N, 8, 16, V); H = th.astype(np.int64).reshape(N, 8)
    F = np.zeros((N, 8, W), np.int64) + np.arange(W); M = np.zeros(N, np.int64); odd = (np.arange(16) % 2 == 1)[:, None]; NONE = 2 ** 20
    qi, gi = np.arange(N)[:, None, None], np.arange(8)[None, :, None]
    for t in range(RO):
        r_old, p_old, f_old = R[..., :G].copy(), P[..., :G].copy(), F[..., :G].copy()
        a = slice(t % QA, V, QA); v = np.arange(t % QA, V, QA); L = len(v)
        c = np.take_along_axis(F, C[..., a].reshape(N, 8, 16 * L), 2)
        xc, rc, pc = [at(w, i).reshape(N, 8, 16, 16, L) for w, i in ((X, np.minimum(c, V - 1)), (R, c), (P, c))]
        xv, rv, pv = [w[..., a][:, :, :, None, :] for w in (X, R, P)]
        c = c.reshape(N, 8, 16, L); ordered = np.any((rv <= pc) | (rc <= pv), axis=2)
        fit = ~ordered & (c < V) & (c % QA != t % QA)
        D = np.where(fit, np.add.reduce(np.abs(xc - xv), axis=2), NONE)
        k = np.argmin(D, axis=2)[:, :, None, :]
        b = np.take_along_axis(c, k, 2)[:, :, 0]; D = np.take_along_axis(D, k, 2)[:, :, 0].astype(np.int64); has = D < NONE; b = np.where(has, b, 0)
        C[..., a] = np.where(ordered & has[:, :, None, :], at(C, b), C[..., a])
        asks = has & (D < H[:, :, None] + (M & 31)[:, None, None]); key = np.where(asks, D * V + v, 2 ** 40)
        best = np.full((N, 8, V), 2 ** 40, np.int64); np.minimum.at(best, (qi, gi, b), key)
        win = asks & (np.take_along_axis(best, b, 2) == key); m = win[:, :, None, :]
        xb, rb, pb, sb = at(X, b), at(R, b), at(P, b), at(S, b)
        X[..., a] = np.where(m, (X[..., a] + xb) >> 1, X[..., a])
        R[..., a] = np.where(m, np.minimum(R[..., a], rb), R[..., a]); P[..., a] = np.where(m, np.maximum(P[..., a], pb), P[..., a])
        S[..., a] = np.where(m & odd, sb, S[..., a])
        i, j, l = np.nonzero(win); F[i, j, b[i, j, l]] = v[l]
        M = np.add.reduce(win.astype(np.int64).reshape(N, -1), axis=1)
        a = slice(t % QB, V, QB); L = len(range(t % QB, V, QB))
        c = np.take_along_axis(F, S[..., a].reshape(N, 8, 16 * L), 2)
        low = np.min(at(R, c).reshape(N, 8, 16, 16, L), axis=3); R[..., a] = np.minimum(R[..., a], low)
        ch = np.any(R[..., :G] != r_old, axis=2) | np.any(P[..., :G] != p_old, axis=2) | (F[..., :G] != f_old)
        go = ch & (np.add.accumulate(ch.astype(np.int64), axis=2) <= CAP)
        for turn, o in ((-1, V), (1, V + G)):
            w = np.roll(go, turn, axis=0); m = w[:, :, None, :]; f = np.roll(F[..., :G], turn, axis=0)
            R[..., o:o + G] = np.where(m, np.roll(R[..., :G], turn, axis=0), R[..., o:o + G])
            P[..., o:o + G] = np.where(m, np.roll(P[..., :G], turn, axis=0), P[..., o:o + G])
            F[..., o:o + G] = np.where(w & (f < G), f + o, F[..., o:o + G])
    return {"yx": X.reshape(N, 128, V).astype(np.float32).astype(BF), "yr": np.ascontiguousarray(R[..., :V]).reshape(N, 128, V).astype(np.float32).astype(BF), "yc": C.reshape(N, 128, V).astype(np.float32)}

@@ -1,0 +1,646 @@
+from concourse.bass import DstId, RemoteDMATransfer
+from concourse.mybir import AluOpType as A, AxisListType, ActivationFunctionType as AF
+
+V, G, W, CAP, RO = 704, 672, 2048, 112, 4
+L = V // 4
+NE = 16 * L
+DUMP = W
+GB_ = 800
+NSV = 64
+V3 = 56
+NR = 16 * 88
+BIGX = 512.0
+WO = 16384.0
+WB = 1048576.0
+TILES = [(0, 0), (0, 1), (1, 0), (1, 1), (2, 0), (2, 1), (3, 0), (3, 1), (0, 2), (1, 2), (2, 2), (3, 2)]
+
+SCRATCH = {}
+
+
+def _declare():
+    bf = [("X", V), ("R", 784), ("P", 784), ("RF", W + L), ("PF", W), ("XF", W), ("XM", V), ("BF", W + L), ("BT", 800), ("UT", 800),
+          ("GR", 2 * GB_), ("GP", 2 * GB_), ("GB", 2 * GB_), ("RVB", NE), ("PVB0", NE), ("PVB1", NE), ("XVB", NE), ("GX", NE), ("AX", NE),
+          ("GQ", NE), ("A1", NE), ("A2", NE), ("BC", NE), ("GA", 2 * NE), ("GS", 2 * NE), ("RST", NR), ("E8", 256), ("IW", 160), ("NI", 128),
+          ("Z1", 144), ("ZO", 144), ("Z0", 144), ("ZN", 144), ("ZB", 144), ("ZS", 144), ("BO", 128), ("BN", 128), ("BW", 128), ("BQ", 128),
+          ("SW", 512), ("AE", 256), ("AT", 256), ("LW", 240), ("LM", 256), ("ON", 128), ("KC", 192), ("LC", 12), ("VL", 32), ("C3", G),
+          ("K6", 16), ("FT", 192), ("FR", 192), ("F2", 192), ("G2", 192), ("FE", L), ("FW", L), ("LE", 2 * L), ("YP", 12 * L), ("MN", L),
+          ("MX", L), ("WN", L), ("DX", L), ("OM", L), ("HM", L), ("CH", G), ("CN", G), ("SL", 784), ("SN0", 3 * CAP), ("SN1", 3 * CAP),
+          ("MB", 8), ("LR00", 3 * CAP), ("LR01", 3 * CAP), ("LR10", 3 * CAP), ("LR11", 3 * CAP)]
+    f4 = [("CF", V), ("IO", 800), ("IB", 128), ("I8", 256), ("KO", 32), ("RM", 16), ("WT", 32), ("CJ", 56), ("RK", 192), ("Y8", G),
+          ("KT", 192), ("KS", 192), ("KM", 16), ("NA", 32), ("THR", 16), ("TT", 16), ("DS", L), ("DC", L), ("SO", G), ("DT", 176), ("MC", 4)]
+    i4 = [("CI", V), ("SI", V), ("T8", 2), ("PI", 8), ("YI", 384), ("DI", 16), ("XS", L), ("MI", 8)]
+    u2 = [("CU", V), ("SU", V), ("RL", V), ("LS", 16), ("BL", 16), ("SC", 16), ("FL", 44), ("FG", 100), ("DL", 44), ("IL0", 16), ("IL1", 16),
+          ("LI00", 16), ("LI01", 16), ("LI10", 16), ("LI11", 16)]
+    for lst, d in ((bf, "bfloat16"), (f4, "float32"), (i4, "int32"), (u2, "uint16")):
+        for nm, w in lst:
+            SCRATCH[nm] = ("sbuf", [128, w], d)
+    for b in range(8):
+        SCRATCH["B%d" % b] = ("psum", [128, 512], "float32")
+
+
+_declare()
+SEMAPHORES = ["s_v", "s_s", "s_p", "s_g"] + ["d%d" % i for i in range(9)] + ["ar%d%d" % (i, b) for i in range(8) for b in range(2)] + ["lo%d" % i for i in range(8)]
+
+
+def tracker(g, T):
+    eng = {"v": g.vector, "s": g.scalar, "p": g.tensor, "g": g, "y": g.sync}
+    known = {e: {} for e in eng}
+    cnt = {e: 0 for e in eng}
+    recs = {}
+    total = {}
+
+    def view(name, lo=0, hi=None, st=1, p0=0, p1=128):
+        hi = SCRATCH[name][1][1] if hi is None else hi
+        t = T[name]
+        return (t[p0:p1, lo:hi] if st == 1 else t[p0:p1, lo:hi:st], [(name, lo, hi)])
+
+    def ind(win, off):
+        return (win[0].indirect(off[0]), win[1] + off[1])
+
+    def need(e, rec):
+        sem, val, clock, _ = rec
+        if known[e].get(sem, 0) < val:
+            eng[e].wait_ge(T.sem[sem], val)
+            for k, x in clock.items():
+                if known[e].get(k, 0) < x:
+                    known[e][k] = x
+
+    def depend(e, outs, ins):
+        deps = []
+        for (lst, wr) in ((ins, False), (outs, True)):
+            for v in lst:
+                for (name, lo, hi) in v[1]:
+                    bank = SCRATCH[name][0] == "psum"
+                    for (a, b, w, rec) in recs.get(name, []):
+                        if bank:
+                            if rec[3] != e:
+                                deps.append(rec)
+                        elif a < hi and lo < b and (wr or w):
+                            deps.append(rec)
+        deps.sort(key=lambda r: -r[1])
+        for r in deps:
+            need(e, r)
+
+    def note(rec, outs, ins):
+        for (lst, wr) in ((ins, False), (outs, True)):
+            for v in lst:
+                for (name, lo, hi) in v[1]:
+                    old = recs.get(name, [])
+                    if SCRATCH[name][0] == "psum":
+                        recs[name] = [(0, 512, True, rec)]
+                        continue
+                    if wr:
+                        old = [r for r in old if not (lo <= r[0] and r[1] <= hi)]
+                    else:
+                        old = [r for r in old if not (not r[2] and lo <= r[0] and r[1] <= hi and r[3][3] == rec[3] and rec[3] is not None)]
+                    recs[name] = old + [(lo, hi, wr, rec)]
+
+    def comp(e, fn, out, ins, *args, **kw):
+        depend(e, [out], ins)
+        cnt[e] += 1
+        sem = "s_" + e
+        rec = (sem, cnt[e], dict(known[e]), e)
+        rec[2][sem] = cnt[e]
+        fn(*args, **kw).then_inc(T.sem[sem], 1)
+        total[sem] = cnt[e]
+        note(rec, [out], ins)
+        return rec
+
+    def dma(e, sem, out, in_):
+        o = [out] if len(out) > 1 else []
+        i = [in_] if len(in_) > 1 else []
+        depend(e, o, i)
+        eng[e].dma_start(out[0], in_[0]).then_inc(T.sem[sem], 16)
+        rec = (sem, 16, dict(known[e]), None)
+        rec[2][sem] = 16
+        total[sem] = 16
+        note(rec, o, i)
+
+    def sent(call, sem, val, srcs):
+        depend("g", [], srcs)
+        call()
+        rec = (sem, val, dict(known["g"]), None)
+        rec[2][sem] = val
+        total[sem] = val
+        note(rec, [], srcs)
+
+    def arrives(sem, val, out):
+        total[sem] = val
+        note((sem, val, {sem: val}, None), [out], [])
+
+    def finish():
+        for k in sorted(total):
+            if known["y"].get(k, 0) < total[k]:
+                g.sync.wait_ge(T.sem[k], total[k])
+    return view, ind, comp, dma, sent, arrives, finish, need
+
+
+def rank_program(g, core, T, topo):
+    rank = T.rank_of(core)
+    if rank is None:
+        return
+    n = len(T.cores)
+
+    def shares(c):
+        q, used = T.rank_of(c), {}
+        for d in sorted([T.cores[(q - 1) % n], T.cores[(q + 1) % n]], key=lambda z: len(topo.engines(c, z))):
+            used[d] = [e for e in topo.engines(c, d) if not any(e in x for x in used.values())]
+        return used
+    nb = [(T.cores[(rank - 1) % n], 0), (T.cores[(rank + 1) % n], 1)]
+    eng = shares(core)
+    arrive_n = [len(shares(T.cores[(rank + 1) % n])[core]), len(shares(T.cores[(rank - 1) % n])[core])]
+    local_n = sum(len(x) for x in eng.values())
+
+    view, ind, comp, dma, sent, arrives, finish, need = tracker(g, T)
+    vec, sca, ten = g.vector, g.scalar, g.tensor
+
+    def cp(o, i): comp("v", vec.tensor_copy, o, [i], o[0], i[0])
+    def tt(o, a, b, op): comp("v", vec.tensor_tensor, o, [a, b], o[0], a[0], b[0], op)
+    def ts(o, a, s1, op0, s2=None, op1=None):
+        ins = [a] + [s for s in (s1, s2) if isinstance(s, tuple)]
+        u1 = s1[0] if isinstance(s1, tuple) else s1
+        u2 = s2[0] if isinstance(s2, tuple) else s2
+        if op1 is None:
+            comp("v", vec.tensor_scalar, o, ins, o[0], a[0], u1, None, op0)
+        else:
+            comp("v", vec.tensor_scalar, o, ins, o[0], a[0], u1, u2, op0, op1)
+    def ms(o, c): comp("v", vec.memset, o, [], o[0], c)
+    def scan(o, a, b, init, op0, op1): comp("v", vec.tensor_tensor_scan, o, [a, b], o[0], a[0], b[0], init, op0, op1)
+    def tr(o, i): comp("v", vec.transpose, o, [i], o[0], i[0])
+    def red(o, i): comp("v", vec.tensor_reduce, o, [i], o[0], i[0], AxisListType.X, A.add)
+    def act(o, i, f, bias=0.0): comp("s", sca.activation, o, [i], o[0], i[0], f, bias=bias)
+    def mm(o, l, r, start, stop): return comp("p", ten.matmul, o, [l, r], o[0], l[0], r[0], start, stop)
+    def iota(o, pat, base, cm): comp("g", g.iota, o, [], o[0], pat, base, cm, allow_small_or_imprecise_dtypes=True)
+    def gfill(name, lo, hi, c): iota(view(name, lo, hi), [[0, hi - lo]], c, 0)
+
+    I = view("IW", 16, 144)
+
+    def zq(z, q): return view(z, 15 - q, 143 - q)
+
+    def listed(o, z, name, lo, hi):
+        for q in range(16):
+            mm(o, zq(z, q), view(name, lo + q, hi, 16), q == 0, q == 15)
+
+    def fused(src, dst, arr, lsem):
+        out = []
+        for d, blk in nb:
+            rid, pid = topo.addr(d, core)
+            out.append(RemoteDMATransfer(dst_ids=[DstId(rid=rid, pnc=pid)], dma_engine_mask=sum(1 << e for e in eng[d]),
+                                         remote_sem=T.sem["%s%d" % (arr, blk)], src=src[0], dst=dst(blk)))
+        sent(lambda: g.remote_dma_fused(out, local_sem=T.sem[lsem]), lsem, local_n, [src])
+
+    dma("y", "d0", view("R", 0, V), (T.reach[:],))
+    comp("g", g.iota, view("PI", 0, 1), [], T.PI[:, 0:1], [[0, 1]], 0, 1)
+    iota(view("IO"), [[1, 800]], 0, 0)
+    dma("s", "d1", view("P", 0, V), (T.past[:],))
+    dma("y", "d2", view("CI"), (T.cand[:],))
+    dma("s", "d3", view("X"), (T.x[:],))
+    dma("y", "d4", view("SI"), (T.succ[:],))
+    dma("s", "d5", view("T8", 0, 1, 1, 0, 8), (T.th[:],))
+    fused(view("R", 0, G), lambda b: T.RF[:, V + G * b: V + G * b + G], "ar0", "lo0")
+    fused(view("P", 0, G), lambda b: T.PF[:, V + G * b: V + G * b + G], "ar1", "lo1")
+    for b in range(2):
+        arrives("ar0%d" % b, arrive_n[b], view("RF", V + G * b, V + G * b + G))
+        arrives("ar1%d" % b, arrive_n[b], view("PF", V + G * b, V + G * b + G))
+    iota(view("IB"), [[16, 8], [0, 16]], 0, 0)
+    for h in range(2):
+        iota(view("I8", 128 * h, 128 * h + 128, 1, 0, 8), [[2, 4], [0, 32]], h, -1)
+
+    def ko(i): return view("KO", i, i + 1)
+    def pi(i): return view("PI", i, i + 1)
+    def rm(i): return view("RM", i, i + 1)
+    ts(pi(1), pi(0), 15, A.bitwise_and)
+    ts(pi(2), pi(0), 112, A.bitwise_and)
+    ts(pi(3), pi(0), 4, A.arith_shift_right, 1, A.bitwise_and)
+    ts(pi(4), pi(0), 31, A.bitwise_and)
+    ts(pi(5), pi(0), 1, A.bitwise_and)
+    cp(ko(1), pi(2)); cp(ko(0), pi(1)); cp(ko(2), pi(3)); cp(ko(9), pi(4)); cp(ko(20), pi(5))
+    ts(ko(4), pi(0), 16.0, A.add)
+    ts(ko(5), ko(1), 15.0, A.add)
+    ts(view("IW"), view("IO", 0, 160), ko(4), A.is_equal)
+    ts(view("Z1"), view("IO", 0, 144), ko(5), A.is_equal)
+    ts(view("KC"), view("IO", 0, 192), 0.0, A.mult, ko(0), A.add)
+    ts(view("NI"), I, -1.0, A.mult)
+    ts(view("ZO"), view("Z1"), WO, A.mult)
+    ts(view("KC"), view("KC"), 1.0 / 16, A.mult)
+    gfill("XF", V, W, int(BIGX))
+    gfill("UT", 0, 800, 0)
+    gfill("BF", V, W + L, 0)
+    gfill("R", V, 784, 0); gfill("P", V, 784, 0)
+    gfill("LW", 0, 240, 0); gfill("LM", 0, 256, 0)
+    gfill("RF", W, W + L, 0)
+    gfill("RST", 0, NR, 0)
+    gfill("C3", 0, G, 113)
+    for nm in ("GB", "GR", "GP"):
+        for b in range(2):
+            gfill(nm, GB_ * b + G, GB_ * b + GB_, 0)
+
+    def spread(dst, src, t, by=cp):
+        return [lambda k=k: by(view(dst, k, NE, 16), view(src, t, V, 4)) for k in range(16)]
+
+    def run(l):
+        for f in l:
+            f()
+
+    def xmask(dst, t):
+        ts(view(dst, t, V, 4), view("X", t, V, 4), 0.0, A.mult, BIGX, A.add)
+    cp(view("RF", 0, V), view("R", 0, V))
+    run(spread("RVB", "R", 0))
+    cp(view("PF", 0, V), view("P", 0, V))
+    cp(view("CU", 0, L), view("CI", 0, V, 4))
+    cp(view("XF", 0, V), view("X"))
+    xmask("XF", 0)
+    run(spread("XVB", "X", 0, lambda o, i: act(o, i, AF.Copy)))
+    run(spread("PVB0", "P", 0))
+
+    def key_x_gather(t):
+        act(view("GX"), ind(view("XF"), view("CU", L * t, L * t + L)), AF.Copy)
+
+    def key_start():
+        mm(view("B0", 0, 192), I, view("KC"), True, False)
+
+    def key_x():
+        ch = [(c, min(c + 512, NE), "B%d" % (2 + c // 512)) for c in range(0, NE, 512)]
+        for c, e, b in ch:
+            mm(view(b, 0, e - c), I, view("GX", c, e), True, False)
+            mm(view(b, 0, e - c), view("NI"), view("XVB", c, e), False, True)
+        for c, e, b in ch:
+            act(view("AX", c, e), view(b, 0, e - c), AF.Abs)
+
+    def key_add(z, src, lo, hi, stop=False):
+        for k in range(16):
+            mm(view("B0", lo, hi), zq(z, k), view(src, 16 * lo + k, 16 * hi, 16), False, stop and k == 15)
+
+    def sig_part(which, first, last):
+        z = {"P": "BO", "R": "BN", "BF": "BW"}[which]
+        for h in range(2):
+            mm(view("B%d" % (2 + h), 0, 336), view(z), view(which, 336 * h, 336 * h + 336), first, last)
+
+    def key_bits(t):
+        act(view("BC"), ind(view("BF", 0, W), view("CU", L * t, L * t + L)), AF.Copy)
+    ts(view("BO"), view("IB"), ko(1), A.is_equal)
+    ts(view("BN"), view("BO"), -1.0, A.mult)
+    sig_part("P", True, False); sig_part("R", False, True)
+    for h in range(2):
+        act(view("SO", 336 * h, 336 * h + 336), view("B%d" % (2 + h), 0, 336), AF.Copy)
+    key_x_gather(0)
+    key_start()
+    ts(view("E8", 0, 256, 1, 0, 8), view("I8", 0, 256, 1, 0, 8), 0.0, A.is_equal)
+    ts(view("MI", 4, 5, 1, 0, 8), view("T8", 0, 1, 1, 0, 8), 4080, A.bitwise_and)
+    ts(view("MI", 5, 6, 1, 0, 8), view("T8", 0, 1, 1, 0, 8), 15, A.bitwise_and)
+    cp(view("MB", 4, 6, 1, 0, 8), view("MI", 4, 6, 1, 0, 8))
+    for h in range(2):
+        for i in range(2):
+            mm(view("B1", h, h + 1), view("E8", 128 * h, 128 * h + 128, 1, 0, 8), view("MB", 4 + i, 5 + i, 1, 0, 8), i == 0, i == 1)
+
+    def chain_constants():
+        cp(view("YI", 0, 50), view("IO", 0, 50))
+        for i in range(5):
+            ts(view("YI", 64 + i, 65 + i), pi(0), i, A.arith_shift_right, 1, A.bitwise_and)
+        for i in range(5):
+            ts(view("YI", 80 + 50 * i, 130 + 50 * i), view("YI", 0, 50), i + 1, A.arith_shift_right, 1, A.bitwise_and)
+        ts(view("KO", 24, 29), view("YI", 64, 69), 2.0, A.mult, -1.0, A.add)
+        for i in range(5):
+            ts(view("UT", 5 + i, 800, 16), view("YI", 80 + 50 * i, 130 + 50 * i), 2.0, A.mult, -1.0, A.add)
+        for i in range(5):
+            ts(view("UT", i, 800, 16), view("IO", 0, 50), 0.0, A.mult, ko(24 + i), A.add)
+        tr(view("BT"), view("UT"))
+        cp(view("BF", 0, V), view("BT", 0, V))
+        key_bits(0)
+        ms(view("RK"), 0.0)
+        ms(view("FT"), 0.0); ms(view("F2"), 0.0)
+        ts(view("RK", 0, 192, 16), view("IO", 0, 12), 0.0, A.mult, 2.0 ** 28, A.add)
+        for h in range(2):
+            ts(view("FT", 16 * h + 12, 192, 32), view("IO", 0, 192, 32), ko(9), A.add)
+        for i in (13, 14, 15):
+            ts(view("FT", i, 192, 16), view("IO", 0, 12), 0.0, A.mult, 1.0, A.add)
+        for w in range(2):
+            ts(view("LC", 6 * w, 6 * w + 6), view("IO", 16 * w, 192, 32), ko(0), A.add, 16.0, A.mult)
+        ts(ko(3), ko(2), -1.0, A.mult, 1.0, A.add)
+        ts(view("RM"), view("IO", 0, 16), ko(0), A.is_equal)
+        for h in range(2):
+            for w in range(2):
+                z = 16 - 16 * (h - w)
+                ts(view("SW", 128 * (2 * h + w), 128 * (2 * h + w) + 128), view("IW", z, z + 128), ko(2 if w else 3), A.mult, 16.0, A.mult)
+        ts(ko(6), ko(0), 10.0, A.is_lt)
+        ts(ko(16), rm(13), 256.0, A.mult)
+        tt(ko(17), rm(10), rm(11), A.add)
+        ts(ko(15), ko(6), WB, A.mult)
+        ts(ko(17), ko(17), -256.0, A.mult)
+        ts(view("AT", 0, 128), I, ko(15), A.mult)
+        tt(ko(17), ko(17), rm(12), A.subtract)
+        for d, c in ((-3, ko(16)), (-2, ko(16)), (-1, rm(13)), (3, ko(17))):
+            ts(view("AT", 128, 256), view("IW", 16 - d, 144 - d), c, A.mult)
+            tt(view("AT", 0, 128), view("AT", 0, 128), view("AT", 128, 256), A.add)
+        for h in range(2):
+            ts(view("AE", 128 * h, 128 * h + 128), view("AT", 0, 128), ko(2 if h else 3), A.mult)
+        ms(view("WT"), 0.0)
+        for i in range(10):
+            ms(view("WT", i, i + 1), 2.0 ** (i - 1))
+        tt(view("WT", 16, 32), view("WT", 0, 16), view("RM"), A.mult)
+        red(ko(7), view("WT", 16, 32))
+        ts(view("ZB"), view("Z1"), ko(7), A.mult)
+        ts(view("BQ"), view("BO"), rm(0), A.mult, 512.0, A.mult)
+        ms(view("LW", 112, 128), 512.0)
+        ts(ko(18), ko(4), 75.0, A.is_lt, 512.0, A.mult)
+        ts(ko(19), ko(18), -1.0, A.mult, 512.0, A.add)
+        ts(view("LM", 112, 128), view("LM", 112, 128), ko(18), A.add)
+        ts(view("LM", 128, 144), view("LM", 128, 144), ko(19), A.add)
+        for b in range(6):
+            cp(view("THR", 2 * b, 2 * b + 2), view("B1", 0, 2))
+        ts(view("TT", 0, 12), view("THR", 0, 12), 4096.0, A.min)
+
+    def merge_constants():
+        ts(ko(13), rm(13), -1536.0, A.mult)
+        ts(ko(14), rm(14), -0.5, A.mult)
+        tt(ko(13), ko(13), rm(12), A.subtract)
+        tt(ko(14), ko(14), ko(7), A.add)
+        ts(view("FL"), view("IO", 0, V, 16), ko(0), A.add)
+        tt(ko(13), ko(13), ko(14), A.add)
+        ts(view("VL", 0, 11), view("IO", 0, L, 16), ko(0), A.add)
+        ts(view("ZS"), view("Z1"), ko(13), A.mult)
+        ms(view("VL", 16, 27), float(DUMP))
+        cp(view("SU", 2 * L, 3 * L), view("SI", 2, V, 4))
+        cp(view("CF"), view("CI"))
+        cp(view("XM"), view("X"))
+        ts(view("RST", 0, NR, 16), view("IO", 0, NR // 16), 0.0, A.mult, 512.0, A.add)
+
+    def exchange_constants():
+        ts(view("BW"), view("BO"), ko(7), A.mult, 8192.0, A.mult)
+        ts(view("Y8"), view("IO", 0, G), 8192.0, A.mult, -511.5 * 8192.0, A.add)
+        tt(view("SO"), view("SO"), view("Y8"), A.add)
+        cp(view("CU", L, 2 * L), view("CI", 1, V, 4))
+        ts(view("Z0"), view("Z1"), rm(0), A.mult)
+        ts(view("ZN"), view("Z0"), -1024.0, A.mult)
+        ts(view("CJ", 0, 42), view("IO", 0, G, 16), ko(0), A.add, 112.0 - 1023.0, A.add)
+        ts(view("CJ", 44, 51), view("IO", 0, CAP, 16), ko(0), A.add, 672.0, A.add)
+        ms(view("ON"), 1.0 / 16)
+        ts(view("RL", L, 2 * L), view("IO", 0, V, 4), 1.0, A.add)
+
+    def ghost_constants():
+        for b in range(2):
+            w = GB_ * b
+            cp(view("GB", w, w + G), view("BT", 0, G))
+            cp(view("GP", w, w + G), view("PF", V + G * b, V + G * b + G))
+            cp(view("GR", w, w + G), view("RF", V + G * b, V + G * b + G))
+        for r in (2, 3):
+            cp(view("CU", L * r, L * r + L), view("CI", r, V, 4))
+        for r in (1, 3):
+            cp(view("SU", L * r, L * r + L), view("SI", r, V, 4))
+        for r in (2, 3):
+            ts(view("RL", L * r, L * r + L), view("IO", 0, V, 4), float(r), A.add)
+
+    def spread_p(t):
+        act(view("PVB%d" % (t % 2)), ind(view("P", 0, V), view("RL", L * t, L * t + L)), AF.Copy)
+
+    later = []
+
+    def fill(k):
+        for _ in range(min(k, len(later))):
+            later.pop(0)()
+
+    for t in range(RO):
+        last = t == RO - 1
+        cu = lambda lo, hi: view("CU", L * t + lo, L * t + hi)
+        su = lambda r, lo, hi: view("SU", L * r + lo, L * r + hi)
+        actv = lambda nm: view(nm, t, V, 4)
+        bl = view("BL", 0, 11)
+        pvb = "PVB%d" % (t % 2)
+        s0 = L - NSV if t else L
+        if t:
+            act(view("GQ", 16 * s0, NE), ind(view("PF"), cu(s0, L)), AF.Copy)
+        for lo, hi in ((0, 112), (112, L)):
+            tt(view("A1", 16 * lo, 16 * hi), ind(view("RF", 0, W), cu(lo, hi)), view(pvb, 16 * lo, 16 * hi), A.is_le)
+        for lo, hi in ((0, s0 - 64), (s0 - 64, s0)):
+            tt(view("A2", 16 * lo, 16 * hi), ind(view("PF"), cu(lo, hi)), view("RVB", 16 * lo, 16 * hi), A.is_ge)
+        for c in range(16 * s0, NE, 512):
+            b = "B%d" % (2 + (c // 512) % 6)
+            mm(view(b, 0, 512), I, view("GQ", c, c + 512), True, False)
+            mm(view(b, 0, 512), view("NI"), view("RVB", c, c + 512), False, True)
+            act(view("A2", c, c + 512), view(b, 0, 512), AF.Relu, 1.0)
+        if 0 < t < RO - 1:
+            spread_p(t + 1)
+        key_add("ZO", "A1", 0, 112)
+        if t:
+            key_add("ZO", "A2", s0, L)
+        key_add("ZO", "A1", 112, L)
+        if t == 0:
+            key_x()
+            key_add("Z1", "AX", 0, L)
+        key_add("ZO", "A2", 0, s0 - 64)
+        key_add("ZO", "A2", s0 - 64, s0, True)
+        if t == 0:
+            chain_constants()
+        if not last:
+            later.extend(spread("XVB", "X", t + 1) + spread("RVB", "R", t + 1))
+        fill(8 if t else 0)
+        tr(view("KT"), view("B0", 0, 192))
+        scan(view("KS"), view("RK"), view("KT"), 0.0, A.add, A.min)
+        ts(view("KM", 0, 12), view("KS", 15, 192, 16), 16000.0, A.min)
+        ts(view("DI", 0, 12), view("KM", 0, 12), -0.47, A.add)
+        tt(view("K6", 0, 12), view("KM", 0, 12), view("DI", 0, 12), A.subtract)
+        mm(view("B1", 0, 12), I, view("LC"), True, False)
+        for w in range(2):
+            for h in range(2):
+                j = 128 * (2 * h + w)
+                mm(view("B1", 6 * w, 6 * w + 6), view("SW", j, j + 128), view("K6", h, 12, 2), False, w == 1 and h == 1)
+        cp(view("FT", 10, 192, 16), view("DI", 0, 12))
+        tt(view("FT", 11, 192, 16), view("DI", 0, 12), view("FT", 10, 192, 16), A.subtract)
+        ts(view("OM"), view("B0", 0, L), WO, A.is_ge)
+        tr(view("FR"), view("FT"))
+        for w in range(2):
+            cp(view("LS", w, 12, 2), view("B1", 6 * w, 6 * w + 6))
+        tt(view("FE"), ind(view("BC"), view("LS", 0, 11)), view("FR", 0, L), A.add)
+        mm(view("B6", 0, L), view("AE", 0, 128), view("FE"), True, True)
+        mm(view("B7", 0, L), view("AE", 128, 256), view("FE"), True, True)
+        cp(view("LE", 0, L), view("B6", 0, L))
+        act(view("LE", L, 2 * L), view("B7", 0, L), AF.Copy)
+        listed(view("B0", 0, 11), "ZB", "FE", 0, L)
+        tt(view("NA", 0, 12), view("KM", 0, 12), view("TT", 0, 12), A.is_ge)
+        ts(view("NA", 16, 28), view("KM", 0, 12), 4096.0, A.is_ge, 2.0, A.mult)
+        cp(view("DS"), actv("SI"))
+        tt(view("F2", 0, 192, 16), view("NA", 0, 12), view("NA", 16, 28), A.add)
+        tr(view("G2"), view("F2"))
+        fill(4 if t else 0)
+        done = {}
+        for i in (0, 1, 2, 3, 4, 5, 6, 7, 8, 10, 9, 11):
+            a, j = TILES[i]
+            c = (0, 117, 234)[j]
+            if i in (9, 11):
+                need("p", done[i - 1])
+            done[i] = mm(view("B%d" % (2 + i // 2), L * (i % 2), L * (i % 2) + L, 1, 0, 118), view("LE", c, c + 118, 1, 32 * a, 32 * a + 32),
+                         view("FE", 0, L, 1, 32 * a, 32 * a + 32), True, True)
+        ts(bl, view("B0", 0, 11), 511.5, A.add)
+        mm(view("B0", 64, 64 + L), view("BQ"), view("G2", 0, L), True, True)
+        tt(view("MN"), ind(view("R"), bl), view("RVB", 0, NE, 16), A.min)
+        mm(view("B1", 0, L), I, view("MN"), True, False)
+        mm(view("B1", 0, L), view("BQ"), view("G2", 0, L), False, False)
+        for b in range(6):
+            o = view("YP", 352 * b, 352 * b + 352, 1, 0, 118)
+            i = view("B%d" % (2 + b), 0, 352, 1, 0, 118)
+            if b % 2 == 1:
+                ts(o, i, 10 * WB, A.is_gt)
+            else:
+                act(o, i, AF.Relu, -10 * WB)
+            for i in (2 * b, 2 * b + 1):
+                a, j = TILES[i]
+                if j == 1:
+                    l = view("LM", 112 - 32 * a, 240 - 32 * a, 1, 0, 118)
+                else:
+                    k = 112 - 16 * (2 * a + j // 2)
+                    l = view("LW", k, k + 128, 1, 0, 118)
+                mm(view("B1", 0, L), l, view("YP", L * i, L * i + L, 1, 0, 118), False, i == 11)
+        if t == 0:
+            merge_constants()
+        ts(view("HM"), view("B0", 64, 64 + L), 1000.0, A.is_lt)
+        tt(view("DS"), ind(view("SI"), bl), view("DS"), A.subtract)
+        ts(view("DS"), view("DS"), ko(20), A.mult)
+        tt(view("MX"), ind(view("P"), bl), view(pvb, 0, NE, 16), A.max)
+        fill(10 if t else 0)
+
+        def candidates():
+            cp(view("DC"), actv("CF"))
+            tt(view("HM"), view("HM"), view("OM"), A.mult)
+            tt(view("DC"), ind(view("CF"), bl), view("DC"), A.subtract)
+            tt(view("DC"), view("DC"), view("HM"), A.mult)
+            tt(actv("CF"), actv("CF"), view("DC"), A.add)
+
+        def halves():
+            tt(view("XS"), ind(view("XM"), bl), actv("X"), A.add)
+            ts(view("XS"), view("XS"), 1, A.arith_shift_right)
+            tt(view("DX"), view("XS"), actv("X"), A.subtract)
+
+        def features():
+            tt(view("DX"), view("DX"), view("WN"), A.mult)
+            tt(actv("X"), actv("X"), view("DX"), A.add)
+        if last:
+            candidates()
+            dma("y", "d8", (T.yc[:],), view("CF"))
+            halves()
+        mm(view("B0", 0, 11), I, view("VL", 0, 11), True, False)
+        mm(view("B0", 0, 11), I, view("VL", 16, 27), False, False)
+        ts(view("WN"), view("B1", 0, L), 512.0, A.is_lt)
+        tt(actv("R"), view("B1", 0, L), actv("R"), A.min)
+        tt(view("FW"), view("FE"), view("WN"), A.mult)
+        act(view("RF", 0, V), ind(view("R", 0, V), view("FL")), AF.Copy)
+        for q in range(16):
+            mm(view("B0", 0, 11), zq("ZS", q), view("FW", q, L, 16), False, q == 15)
+        tt(view("DS"), view("DS"), view("WN"), A.mult)
+        tt(actv("SI"), actv("SI"), view("DS"), A.add)
+        cp(view("SC", 0, 11), view("B0", 0, 11))
+        cp(su(t, 0, L), actv("SI"))
+        cp(ind(view("RF"), view("SC", 0, 11)), actv("R"))
+        o = (t + 2) % 4
+        rf = view("RF", 0, W)
+        for lo, hi in ((0, 88), (88, L)):
+            act(view("GA", 16 * lo, 16 * hi), ind(rf, su(o, lo, hi)), AF.Copy)
+        for lo, hi in ((V3, 112), (112, L)):
+            act(view("GA", NE + 16 * lo, NE + 16 * hi), ind(rf, su(t, lo, hi)), AF.Copy)
+        cp(view("GA", NE, NE + 16 * V3), ind(rf, su(t, 0, V3)))
+
+        def low(r, lo, hi):
+            a, e = (NE if r == t else 0) + 16 * lo, (NE if r == t else 0) + 16 * hi
+            scan(view("GS", a, e), view("RST", 0, e - a), view("GA", a, e), 0.0, A.add, A.min)
+            z = view("R", r + 4 * lo, r + 4 * hi - 3, 4)
+            tt(z, view("GS", a + 15, e, 16), z, A.min)
+        if not last:
+            cp(ind(view("BF"), view("SC", 0, 11)), view("BT", t, V, 4))
+            listed(view("B0", 0, 44), "ZB", "BF", 0, V)
+            tt(view("MX"), view("MX"), view("WN"), A.mult)
+            tt(actv("P"), actv("P"), view("MX"), A.max)
+            if t == 0:
+                exchange_constants()
+            sig_part("P", True, False)
+            sig_part("BF", False, False)
+        low(t, 0, V3)
+        low(o, 0, 88)
+        if not last:
+            ts(view("FL"), view("B0", 0, 44), 511.5, A.add)
+        low(o, 88, L)
+        low(t, V3, 112)
+        if last:
+            features()
+            dma("y", "d7", (T.yx[:],), view("X"))
+        low(t, 112, L)
+        if last:
+            dma("y", "d6", (T.yr[:],), view("R", 0, V))
+            break
+        sig_part("R", False, True)
+        for h in range(2):
+            tt(view("CH", 336 * h, 336 * h + 336), view("B%d" % (2 + h), 0, 336), view("SO", 336 * h, 336 * h + 336), A.not_equal)
+        for h in range(2):
+            act(view("SO", 336 * h, 336 * h + 336), view("B%d" % (2 + h), 0, 336), AF.Copy)
+        act(view("PF", 0, V), ind(view("P", 0, V), view("FL")), AF.Copy)
+        for q in range(16):
+            mm(view("B1", 0, 42), zq("ZN", q), view("CH", q, G, 16), q == 0, False)
+        scan(view("CN"), view("CH"), view("C3"), 0.0, A.add, A.min)
+        for q in range(16):
+            mm(view("B1", 0, 42), zq("Z0", q), view("CN", q, G, 16), False, q == 15)
+        halves()
+        features()
+        cp(actv("XM"), actv("X"))
+        xmask("XM", t + 1)
+        act(view("XF", 0, V), ind(view("XM"), view("FL")), AF.Copy)
+        key_x_gather(t + 1)
+        key_bits(t + 1)
+        cp(view("SL", 0, CAP), view("BT", G, G + CAP))
+        ts(view("DT", 0, 42), view("B1", 0, 42), -911.0, A.is_ge, 4096.0, A.mult)
+        tt(view("DT", 44, 86), view("B1", 0, 42), view("DT", 0, 42), A.add)
+        tt(view("DT", 88, 130), view("DT", 44, 86), view("CJ", 0, 42), A.min)
+        ts(view("DL", 0, 42), view("DT", 88, 130), 1023.0, A.add)
+        cp(ind(view("SL"), view("DL", 0, 42)), view("BT", 0, G))
+        e = t % 2
+        il, sn = "IL%d" % e, "SN%d" % e
+        jl = view(il, 0, 7)
+        listed(view("B1", 0, 7), "ZB", "SL", 0, CAP)
+        ms(view(il, 7, 8), 0); ms(view(il, 15, 16), 0)
+        fill(2)
+        ts(jl, view("B1", 0, 7), 511.5, A.add)
+        ts(view("DT", 132, 139), view("B1", 0, 7), 511.5, A.add)
+        cp(view(sn, 2 * CAP, 3 * CAP), ind(view("BF"), jl))
+        listed(view("B1", 0, 7), "ZB", sn, 2 * CAP, 3 * CAP)
+        cp(view(sn, 0, CAP), ind(view("R"), jl))
+        cp(view(sn, CAP, 2 * CAP), ind(view("P"), jl))
+        fused(view(sn), lambda b: T["LR%d%d" % (e, b)][:], "ar%d" % (2 + 2 * t), "lo%d" % (2 + 2 * t))
+        tt(view("DT", 140, 147), view("CJ", 44, 51), view("DT", 132, 139), A.subtract)
+        ts(view("DT", 148, 155), view("B1", 0, 7), 160.0, A.is_ge)
+        tt(view("DT", 148, 155), view("DT", 148, 155), view("DT", 140, 147), A.mult)
+        tt(view("DT", 148, 155), view("DT", 148, 155), view("DT", 132, 139), A.add)
+        cp(view(il, 8, 15), view("DT", 148, 155))
+        fused(view(il), lambda b: T["LI%d%d" % (e, b)][:], "ar%d" % (3 + 2 * t), "lo%d" % (3 + 2 * t))
+        for b in range(2):
+            arrives("ar%d%d" % (2 + 2 * t, b), arrive_n[b], view("LR%d%d" % (e, b)))
+            arrives("ar%d%d" % (3 + 2 * t, b), arrive_n[b], view("LI%d%d" % (e, b)))
+        red(view("MC", 0, 1), view("WN"))
+        cp(view("MB", 0, 1), view("MC", 0, 1))
+        mm(view("B1", 0, 1), view("ON"), view("MB", 0, 1), True, True)
+        cp(view("RF", 0, V), ind(view("R", 0, V), view("FL")))
+        while len(later) > 16:
+            fill(1)
+        key_start()
+        key_x()
+        if t == 0:
+            spread_p(1)
+        cp(view("MI", 0, 1), view("B1", 0, 1))
+        candidates()
+        ts(view("MI", 1, 2), view("MI", 0, 1), 31, A.bitwise_and)
+        cp(view("MC", 1, 2), view("MI", 1, 2))
+        ts(view("TT", 0, 12), view("THR", 0, 12), view("MC", 1, 2), A.add, 4096.0, A.min)
+        if t == 0:
+            ghost_constants()
+        fill(99)
+        def taken(nm, lo, c):
+            for b in range(2):
+                cp(ind(view(nm, GB_ * b, GB_ * b + GB_), view("LI%d%d" % (e, b), lo, lo + 7)), view("LR%d%d" % (e, b), c, c + CAP))
+        taken("GB", 8, 2 * CAP)
+        for q in range(16):
+            mm(view("B1", 0, 92), zq("ZB", q), view("GB", q, 1472, 16), q == 0, q == 15)
+        key_add("Z1", "AX", 0, L)
+        taken("GP", 0, CAP)
+        ts(view("FG", 0, 92), view("B1", 0, 92), 511.5, A.add)
+        taken("GR", 0, 0)
+        for b in range(2):
+            w, f = (GB_ * b, GB_ * b + GB_), view("FG", 50 * b, 50 * b + 42)
+            act(view("PF", V + G * b, V + G * b + G), ind(view("GP", *w), f), AF.Copy)
+            cp(view("RF", V + G * b, V + G * b + G), ind(view("GR", *w), f))
+    finish()

@@ -6,8 +6,8 @@ L = V // 4
 NE = 16 * L
 DUMP = W
 GB_ = 800
-NSV = 64
-V3 = 56
+XC = 3
+V3, VL3 = 56, 64
 NR = 16 * 88
 BIGX = 512.0
 WO = 16384.0
@@ -19,8 +19,8 @@ SCRATCH = {}
 
 def _declare():
     bf = [("X", V), ("R", 784), ("P", 784), ("RF", W + L), ("PF", W), ("XF", W), ("XM", V), ("BF", W + L), ("BT", 800), ("UT", 800),
-          ("GR", 2 * GB_), ("GP", 2 * GB_), ("GB", 2 * GB_), ("RVB", NE), ("PVB0", NE), ("PVB1", NE), ("XVB", NE), ("GX", NE), ("AX", NE),
-          ("GQ", NE), ("A1", NE), ("A2", NE), ("BC", NE), ("GA", 2 * NE), ("GS", 2 * NE), ("RST", NR), ("E8", 256), ("IW", 160), ("NI", 128),
+          ("GR", 2 * GB_), ("GP", 2 * GB_), ("GB", 2 * GB_), ("RVB0", NE), ("RVB1", NE), ("PVB0", NE), ("PVB1", NE), ("XVB", NE), ("GX", NE),
+          ("AX", NE), ("A1", NE), ("A2", NE), ("BC", NE), ("GA", 2 * NE), ("GS", 2 * NE), ("RST", NR), ("E8", 256), ("IW", 160), ("NI", 128),
           ("Z1", 144), ("ZO", 144), ("Z0", 144), ("ZN", 144), ("ZB", 144), ("ZS", 144), ("BO", 128), ("BN", 128), ("BW", 128), ("BQ", 128),
           ("SW", 512), ("AE", 256), ("AT", 256), ("LW", 240), ("LM", 256), ("ON", 128), ("KC", 192), ("LC", 12), ("VL", 32), ("C3", G),
           ("K6", 16), ("FT", 192), ("FR", 192), ("F2", 192), ("G2", 192), ("FE", L), ("FW", L), ("LE", 2 * L), ("YP", 12 * L), ("MN", L),
@@ -39,7 +39,7 @@ def _declare():
 
 
 _declare()
-SEMAPHORES = ["s_v", "s_s", "s_p", "s_g"] + ["d%d" % i for i in range(9)] + ["ar%d%d" % (i, b) for i in range(8) for b in range(2)] + ["lo%d" % i for i in range(8)]
+SEMAPHORES = ["s_v", "s_s", "s_p", "s_g"] + ["d%d" % i for i in range(15)] + ["ar%d%d" % (i, b) for i in range(8) for b in range(2)] + ["lo%d" % i for i in range(8)]
 
 
 def tracker(g, T):
@@ -225,6 +225,10 @@ def rank_program(g, core, T, topo):
     ts(view("KC"), view("KC"), 1.0 / 16, A.mult)
     gfill("XF", V, W, int(BIGX))
     gfill("UT", 0, 800, 0)
+    for nm, w in (("RK", 192), ("FT", 192), ("F2", 192), ("WT", 16)):
+        gfill(nm, 0, w, 0)
+    for i in range(10):
+        gfill("WT", i, i + 1, 2 ** i)
     gfill("BF", V, W + L, 0)
     gfill("R", V, 784, 0); gfill("P", V, 784, 0)
     gfill("LW", 0, 240, 0); gfill("LM", 0, 256, 0)
@@ -235,8 +239,11 @@ def rank_program(g, core, T, topo):
         for b in range(2):
             gfill(nm, GB_ * b + G, GB_ * b + GB_, 0)
 
-    def spread(dst, src, t, by=cp):
-        return [lambda k=k: by(view(dst, k, NE, 16), view(src, t, V, 4)) for k in range(16)]
+    def spread(dst, src, t):
+        return [lambda k=k: cp(view(dst, k, NE, 16), view(src, t, V, 4)) for k in range(16)]
+
+    def spread_s(dst, src, t):
+        act(view(dst), ind(view(src, 0, V), view("RL", L * t, L * t + L)), AF.Copy)
 
     def run(l):
         for f in l:
@@ -244,13 +251,15 @@ def rank_program(g, core, T, topo):
 
     def xmask(dst, t):
         ts(view(dst, t, V, 4), view("X", t, V, 4), 0.0, A.mult, BIGX, A.add)
+    for r in range(2):
+        ts(view("RL", L * r, L * r + L), view("IO", 0, V, 4), float(r), A.add)
     cp(view("RF", 0, V), view("R", 0, V))
-    run(spread("RVB", "R", 0))
+    run(spread("RVB0", "R", 0))
     cp(view("PF", 0, V), view("P", 0, V))
     cp(view("CU", 0, L), view("CI", 0, V, 4))
     cp(view("XF", 0, V), view("X"))
     xmask("XF", 0)
-    run(spread("XVB", "X", 0, lambda o, i: act(o, i, AF.Copy)))
+    spread_s("XVB", "X", 0)
     run(spread("PVB0", "P", 0))
 
     def key_x_gather(t):
@@ -259,31 +268,34 @@ def rank_program(g, core, T, topo):
     def key_start():
         mm(view("B0", 0, 192), I, view("KC"), True, False)
 
-    def key_x():
-        ch = [(c, min(c + 512, NE), "B%d" % (2 + c // 512)) for c in range(0, NE, 512)]
-        for c, e, b in ch:
+    CH = [(c, min(c + 512, NE), "B%d" % (2 + c // 512)) for c in range(0, NE, 512)]
+
+    def x_diff(lo, hi):
+        for c, e, b in CH[lo:hi]:
             mm(view(b, 0, e - c), I, view("GX", c, e), True, False)
             mm(view(b, 0, e - c), view("NI"), view("XVB", c, e), False, True)
-        for c, e, b in ch:
+
+    def x_size(lo, hi):
+        for c, e, b in CH[lo:hi]:
             act(view("AX", c, e), view(b, 0, e - c), AF.Abs)
 
     def key_add(z, src, lo, hi, stop=False):
         for k in range(16):
             mm(view("B0", lo, hi), zq(z, k), view(src, 16 * lo + k, 16 * hi, 16), False, stop and k == 15)
 
-    def sig_part(which, first, last):
+    def sig_part(which, first, last, bank=2):
         z = {"P": "BO", "R": "BN", "BF": "BW"}[which]
         for h in range(2):
-            mm(view("B%d" % (2 + h), 0, 336), view(z), view(which, 336 * h, 336 * h + 336), first, last)
+            mm(view("B%d" % (bank + h), 0, 336), view(z), view(which, 336 * h, 336 * h + 336), first, last)
 
     def key_bits(t):
         act(view("BC"), ind(view("BF", 0, W), view("CU", L * t, L * t + L)), AF.Copy)
     ts(view("BO"), view("IB"), ko(1), A.is_equal)
     ts(view("BN"), view("BO"), -1.0, A.mult)
-    sig_part("P", True, False); sig_part("R", False, True)
-    for h in range(2):
-        act(view("SO", 336 * h, 336 * h + 336), view("B%d" % (2 + h), 0, 336), AF.Copy)
+    sig_part("P", True, False, 6); sig_part("R", False, True, 6)
     key_x_gather(0)
+    for h in range(2):
+        act(view("SO", 336 * h, 336 * h + 336), view("B%d" % (6 + h), 0, 336), AF.Copy)
     key_start()
     ts(view("E8", 0, 256, 1, 0, 8), view("I8", 0, 256, 1, 0, 8), 0.0, A.is_equal)
     ts(view("MI", 4, 5, 1, 0, 8), view("T8", 0, 1, 1, 0, 8), 4080, A.bitwise_and)
@@ -294,6 +306,8 @@ def rank_program(g, core, T, topo):
             mm(view("B1", h, h + 1), view("E8", 128 * h, 128 * h + 128, 1, 0, 8), view("MB", 4 + i, 5 + i, 1, 0, 8), i == 0, i == 1)
 
     def chain_constants():
+        for b in range(6):
+            cp(view("THR", 2 * b, 2 * b + 2), view("B1", 0, 2))
         cp(view("YI", 0, 50), view("IO", 0, 50))
         for i in range(5):
             ts(view("YI", 64 + i, 65 + i), pi(0), i, A.arith_shift_right, 1, A.bitwise_and)
@@ -307,8 +321,7 @@ def rank_program(g, core, T, topo):
         tr(view("BT"), view("UT"))
         cp(view("BF", 0, V), view("BT", 0, V))
         key_bits(0)
-        ms(view("RK"), 0.0)
-        ms(view("FT"), 0.0); ms(view("F2"), 0.0)
+        spread_s("PVB1", "P", 1)
         ts(view("RK", 0, 192, 16), view("IO", 0, 12), 0.0, A.mult, 2.0 ** 28, A.add)
         for h in range(2):
             ts(view("FT", 16 * h + 12, 192, 32), view("IO", 0, 192, 32), ko(9), A.add)
@@ -334,20 +347,18 @@ def rank_program(g, core, T, topo):
             tt(view("AT", 0, 128), view("AT", 0, 128), view("AT", 128, 256), A.add)
         for h in range(2):
             ts(view("AE", 128 * h, 128 * h + 128), view("AT", 0, 128), ko(2 if h else 3), A.mult)
-        ms(view("WT"), 0.0)
-        for i in range(10):
-            ms(view("WT", i, i + 1), 2.0 ** (i - 1))
         tt(view("WT", 16, 32), view("WT", 0, 16), view("RM"), A.mult)
-        red(ko(7), view("WT", 16, 32))
+        red(ko(10), view("WT", 16, 32))
+        ts(ko(7), ko(10), 0.5, A.mult)
         ts(view("ZB"), view("Z1"), ko(7), A.mult)
+
+    def rival_constants():
         ts(view("BQ"), view("BO"), rm(0), A.mult, 512.0, A.mult)
         ms(view("LW", 112, 128), 512.0)
         ts(ko(18), ko(4), 75.0, A.is_lt, 512.0, A.mult)
         ts(ko(19), ko(18), -1.0, A.mult, 512.0, A.add)
         ts(view("LM", 112, 128), view("LM", 112, 128), ko(18), A.add)
         ts(view("LM", 128, 144), view("LM", 128, 144), ko(19), A.add)
-        for b in range(6):
-            cp(view("THR", 2 * b, 2 * b + 2), view("B1", 0, 2))
         ts(view("TT", 0, 12), view("THR", 0, 12), 4096.0, A.min)
 
     def merge_constants():
@@ -375,23 +386,20 @@ def rank_program(g, core, T, topo):
         ts(view("CJ", 0, 42), view("IO", 0, G, 16), ko(0), A.add, 112.0 - 1023.0, A.add)
         ts(view("CJ", 44, 51), view("IO", 0, CAP, 16), ko(0), A.add, 672.0, A.add)
         ms(view("ON"), 1.0 / 16)
-        ts(view("RL", L, 2 * L), view("IO", 0, V, 4), 1.0, A.add)
+        ts(view("RL", 2 * L, 3 * L), view("IO", 0, V, 4), 2.0, A.add)
 
     def ghost_constants():
         for b in range(2):
             w = GB_ * b
-            cp(view("GB", w, w + G), view("BT", 0, G))
-            cp(view("GP", w, w + G), view("PF", V + G * b, V + G * b + G))
-            cp(view("GR", w, w + G), view("RF", V + G * b, V + G * b + G))
-        for r in (2, 3):
-            cp(view("CU", L * r, L * r + L), view("CI", r, V, 4))
-        for r in (1, 3):
-            cp(view("SU", L * r, L * r + L), view("SI", r, V, 4))
-        for r in (2, 3):
-            ts(view("RL", L * r, L * r + L), view("IO", 0, V, 4), float(r), A.add)
+            for i, (nm, src) in enumerate((("GR", view("RF", V + G * b, V + G * b + G)), ("GP", view("PF", V + G * b, V + G * b + G)), ("GB", view("BT", 0, G)))):
+                dma("y", "d%d" % (9 + 3 * b + i), view(nm, w, w + G), src)
 
-    def spread_p(t):
-        act(view("PVB%d" % (t % 2)), ind(view("P", 0, V), view("RL", L * t, L * t + L)), AF.Copy)
+    def list_constants(t):
+        out = [lambda: cp(view("CU", L * t + L, L * t + 2 * L), view("CI", t + 1, V, 4))]
+        if t == 1:
+            out.append(lambda: cp(view("SU", 3 * L, 4 * L), view("SI", 3, V, 4)))
+            out.append(lambda: ts(view("RL", 3 * L, 4 * L), view("IO", 0, V, 4), 3.0, A.add))
+        return out
 
     later = []
 
@@ -405,35 +413,31 @@ def rank_program(g, core, T, topo):
         su = lambda r, lo, hi: view("SU", L * r + lo, L * r + hi)
         actv = lambda nm: view(nm, t, V, 4)
         bl = view("BL", 0, 11)
-        pvb = "PVB%d" % (t % 2)
-        s0 = L - NSV if t else L
-        if t:
-            act(view("GQ", 16 * s0, NE), ind(view("PF"), cu(s0, L)), AF.Copy)
+        pvb, rvb = "PVB%d" % (t % 2), "RVB%d" % (t % 2)
         for lo, hi in ((0, 112), (112, L)):
             tt(view("A1", 16 * lo, 16 * hi), ind(view("RF", 0, W), cu(lo, hi)), view(pvb, 16 * lo, 16 * hi), A.is_le)
-        for lo, hi in ((0, s0 - 64), (s0 - 64, s0)):
-            tt(view("A2", 16 * lo, 16 * hi), ind(view("PF"), cu(lo, hi)), view("RVB", 16 * lo, 16 * hi), A.is_ge)
-        for c in range(16 * s0, NE, 512):
-            b = "B%d" % (2 + (c // 512) % 6)
-            mm(view(b, 0, 512), I, view("GQ", c, c + 512), True, False)
-            mm(view(b, 0, 512), view("NI"), view("RVB", c, c + 512), False, True)
-            act(view("A2", c, c + 512), view(b, 0, 512), AF.Relu, 1.0)
+        for lo, hi in ((0, 112), (112, L)):
+            tt(view("A2", 16 * lo, 16 * hi), ind(view("PF"), cu(lo, hi)), view(rvb, 16 * lo, 16 * hi), A.is_ge)
         if 0 < t < RO - 1:
-            spread_p(t + 1)
+            spread_s("PVB%d" % ((t + 1) % 2), "P", t + 1)
+            spread_s("RVB%d" % ((t + 1) % 2), "R", t + 1)
         key_add("ZO", "A1", 0, 112)
         if t:
-            key_add("ZO", "A2", s0, L)
+            key_add("Z1", "AX", 32 * XC, L)
         key_add("ZO", "A1", 112, L)
         if t == 0:
-            key_x()
+            x_diff(0, 6)
+            x_size(0, 6)
             key_add("Z1", "AX", 0, L)
-        key_add("ZO", "A2", 0, s0 - 64)
-        key_add("ZO", "A2", s0 - 64, s0, True)
+        key_add("ZO", "A2", 0, 112)
+        key_add("ZO", "A2", 112, L, True)
         if t == 0:
             chain_constants()
+            ghost_constants()
         if not last:
-            later.extend(spread("XVB", "X", t + 1) + spread("RVB", "R", t + 1))
-        fill(8 if t else 0)
+            later.extend(list_constants(t) if t else [])
+            later.extend(spread("XVB", "X", t + 1))
+        fill(8)
         tr(view("KT"), view("B0", 0, 192))
         scan(view("KS"), view("RK"), view("KT"), 0.0, A.add, A.min)
         ts(view("KM", 0, 12), view("KS", 15, 192, 16), 16000.0, A.min)
@@ -456,12 +460,14 @@ def rank_program(g, core, T, topo):
         cp(view("LE", 0, L), view("B6", 0, L))
         act(view("LE", L, 2 * L), view("B7", 0, L), AF.Copy)
         listed(view("B0", 0, 11), "ZB", "FE", 0, L)
+        if t == 0:
+            rival_constants()
         tt(view("NA", 0, 12), view("KM", 0, 12), view("TT", 0, 12), A.is_ge)
         ts(view("NA", 16, 28), view("KM", 0, 12), 4096.0, A.is_ge, 2.0, A.mult)
         cp(view("DS"), actv("SI"))
         tt(view("F2", 0, 192, 16), view("NA", 0, 12), view("NA", 16, 28), A.add)
         tr(view("G2"), view("F2"))
-        fill(4 if t else 0)
+        fill(4)
         done = {}
         for i in (0, 1, 2, 3, 4, 5, 6, 7, 8, 10, 9, 11):
             a, j = TILES[i]
@@ -472,7 +478,7 @@ def rank_program(g, core, T, topo):
                          view("FE", 0, L, 1, 32 * a, 32 * a + 32), True, True)
         ts(bl, view("B0", 0, 11), 511.5, A.add)
         mm(view("B0", 64, 64 + L), view("BQ"), view("G2", 0, L), True, True)
-        tt(view("MN"), ind(view("R"), bl), view("RVB", 0, NE, 16), A.min)
+        tt(view("MN"), ind(view("R"), bl), view(rvb, 0, NE, 16), A.min)
         mm(view("B1", 0, L), I, view("MN"), True, False)
         mm(view("B1", 0, L), view("BQ"), view("G2", 0, L), False, False)
         for b in range(6):
@@ -496,7 +502,7 @@ def rank_program(g, core, T, topo):
         tt(view("DS"), ind(view("SI"), bl), view("DS"), A.subtract)
         ts(view("DS"), view("DS"), ko(20), A.mult)
         tt(view("MX"), ind(view("P"), bl), view(pvb, 0, NE, 16), A.max)
-        fill(10 if t else 0)
+        fill(10)
 
         def candidates():
             cp(view("DC"), actv("CF"))
@@ -513,15 +519,11 @@ def rank_program(g, core, T, topo):
         def features():
             tt(view("DX"), view("DX"), view("WN"), A.mult)
             tt(actv("X"), actv("X"), view("DX"), A.add)
-        if last:
-            candidates()
-            dma("y", "d8", (T.yc[:],), view("CF"))
-            halves()
         mm(view("B0", 0, 11), I, view("VL", 0, 11), True, False)
         mm(view("B0", 0, 11), I, view("VL", 16, 27), False, False)
         ts(view("WN"), view("B1", 0, L), 512.0, A.is_lt)
-        tt(actv("R"), view("B1", 0, L), actv("R"), A.min)
         tt(view("FW"), view("FE"), view("WN"), A.mult)
+        tt(actv("R"), view("B1", 0, L), actv("R"), A.min)
         act(view("RF", 0, V), ind(view("R", 0, V), view("FL")), AF.Copy)
         for q in range(16):
             mm(view("B0", 0, 11), zq("ZS", q), view("FW", q, L, 16), False, q == 15)
@@ -532,11 +534,12 @@ def rank_program(g, core, T, topo):
         cp(ind(view("RF"), view("SC", 0, 11)), actv("R"))
         o = (t + 2) % 4
         rf = view("RF", 0, W)
+        v3 = VL3 if last else V3
         for lo, hi in ((0, 88), (88, L)):
             act(view("GA", 16 * lo, 16 * hi), ind(rf, su(o, lo, hi)), AF.Copy)
-        for lo, hi in ((V3, 112), (112, L)):
+        for lo, hi in ((v3, 112), (112, L)):
             act(view("GA", NE + 16 * lo, NE + 16 * hi), ind(rf, su(t, lo, hi)), AF.Copy)
-        cp(view("GA", NE, NE + 16 * V3), ind(rf, su(t, 0, V3)))
+        cp(view("GA", NE, NE + 16 * v3), ind(rf, su(t, 0, v3)))
 
         def low(r, lo, hi):
             a, e = (NE if r == t else 0) + 16 * lo, (NE if r == t else 0) + 16 * hi
@@ -552,15 +555,21 @@ def rank_program(g, core, T, topo):
                 exchange_constants()
             sig_part("P", True, False)
             sig_part("BF", False, False)
-        low(t, 0, V3)
-        low(o, 0, 88)
-        if not last:
-            ts(view("FL"), view("B0", 0, 44), 511.5, A.add)
-        low(o, 88, L)
-        low(t, V3, 112)
+        low(t, 0, v3)
         if last:
+            halves()
             features()
             dma("y", "d7", (T.yx[:],), view("X"))
+        low(o, 0, 88)
+        if last:
+            candidates()
+            dma("y", "d8", (T.yc[:],), view("CF"))
+        else:
+            ts(view("FL"), view("B0", 0, 44), 511.5, A.add)
+        low(o, 88, L)
+        if not last:
+            halves()
+        low(t, v3, 112)
         low(t, 112, L)
         if last:
             dma("y", "d6", (T.yr[:],), view("R", 0, V))
@@ -576,7 +585,6 @@ def rank_program(g, core, T, topo):
         scan(view("CN"), view("CH"), view("C3"), 0.0, A.add, A.min)
         for q in range(16):
             mm(view("B1", 0, 42), zq("Z0", q), view("CN", q, G, 16), False, q == 15)
-        halves()
         features()
         cp(actv("XM"), actv("X"))
         xmask("XM", t + 1)
@@ -596,8 +604,8 @@ def rank_program(g, core, T, topo):
         ms(view(il, 7, 8), 0); ms(view(il, 15, 16), 0)
         fill(2)
         ts(jl, view("B1", 0, 7), 511.5, A.add)
-        ts(view("DT", 132, 139), view("B1", 0, 7), 511.5, A.add)
         cp(view(sn, 2 * CAP, 3 * CAP), ind(view("BF"), jl))
+        ts(view("DT", 132, 139), view("B1", 0, 7), 511.5, A.add)
         listed(view("B1", 0, 7), "ZB", sn, 2 * CAP, 3 * CAP)
         cp(view(sn, 0, CAP), ind(view("R"), jl))
         cp(view(sn, CAP, 2 * CAP), ind(view("P"), jl))
@@ -615,32 +623,38 @@ def rank_program(g, core, T, topo):
         cp(view("MB", 0, 1), view("MC", 0, 1))
         mm(view("B1", 0, 1), view("ON"), view("MB", 0, 1), True, True)
         cp(view("RF", 0, V), ind(view("R", 0, V), view("FL")))
-        while len(later) > 16:
-            fill(1)
-        key_start()
-        key_x()
+        fill(99)
         if t == 0:
-            spread_p(1)
+            spread_s("RVB1", "R", 1)
+        key_start()
+        x_diff(0, XC)
+        x_size(0, XC)
         cp(view("MI", 0, 1), view("B1", 0, 1))
         candidates()
         ts(view("MI", 1, 2), view("MI", 0, 1), 31, A.bitwise_and)
         cp(view("MC", 1, 2), view("MI", 1, 2))
         ts(view("TT", 0, 12), view("THR", 0, 12), view("MC", 1, 2), A.add, 4096.0, A.min)
-        if t == 0:
-            ghost_constants()
-        fill(99)
+
         def taken(nm, lo, c):
             for b in range(2):
                 cp(ind(view(nm, GB_ * b, GB_ * b + GB_), view("LI%d%d" % (e, b), lo, lo + 7)), view("LR%d%d" % (e, b), c, c + CAP))
+
+        def renamed(dst, nm, b):
+            return view(dst, V + G * b, V + G * b + G), ind(view(nm, GB_ * b, GB_ * b + GB_), view("FG", 50 * b, 50 * b + 42))
         taken("GB", 8, 2 * CAP)
         for q in range(16):
             mm(view("B1", 0, 92), zq("ZB", q), view("GB", q, 1472, 16), q == 0, q == 15)
-        key_add("Z1", "AX", 0, L)
+        x_diff(XC, 6)
+        key_add("Z1", "AX", 0, 32 * XC)
+        taken("GR", 0, 0)
         taken("GP", 0, CAP)
         ts(view("FG", 0, 92), view("B1", 0, 92), 511.5, A.add)
-        taken("GR", 0, 0)
+        cp(*renamed("RF", "GR", 0))
+        if t:
+            act(*renamed("RF", "GR", 1), AF.Copy)
+        else:
+            cp(*renamed("RF", "GR", 1))
         for b in range(2):
-            w, f = (GB_ * b, GB_ * b + GB_), view("FG", 50 * b, 50 * b + 42)
-            act(view("PF", V + G * b, V + G * b + G), ind(view("GP", *w), f), AF.Copy)
-            cp(view("RF", V + G * b, V + G * b + G), ind(view("GR", *w), f))
+            act(*renamed("PF", "GP", b), AF.Copy)
+        x_size(XC, 6)
     finish()

from concourse.bass import DstId, RemoteDMATransfer
from concourse.mybir import AluOpType as A, AxisListType, ActivationFunctionType as AF

V, G, W, CAP, RO = 704, 672, 2048, 112, 4
L = V // 4
NE = 16 * L
DUMP = W
GB_ = 800
XC = 3
V3, VL3 = 56, 64
NR = 16 * 88
BIGX = 512.0
WO = 16384.0
WB = 1048576.0
TILES = [(0, 0), (0, 1), (1, 0), (1, 1), (2, 0), (2, 1), (3, 0), (3, 1), (0, 2), (1, 2), (2, 2), (3, 2)]

SCRATCH = {}


def _declare():
    bf = [("X", V), ("R", 784), ("P", 784), ("RF", W + L), ("PF", W), ("XF", W), ("XM", V), ("BF", W + L), ("BT", 800), ("UT", 800),
          ("GR", 2 * GB_), ("GP", 2 * GB_), ("GB", 2 * GB_), ("RVB0", NE), ("RVB1", NE), ("PVB0", NE), ("PVB1", NE), ("XVB", NE), ("GX", NE),
          ("AX", NE), ("A1", NE), ("A2", NE), ("BC", NE), ("GA", 2 * NE), ("GS", 2 * NE), ("RST", NR), ("E8", 256), ("IW", 160), ("NI", 128),
          ("Z1", 144), ("ZO", 144), ("Z0", 144), ("ZN", 144), ("ZB", 144), ("ZS", 144), ("BO", 128), ("BN", 128), ("BW", 128), ("BQ", 128),
          ("SW", 512), ("AE", 256), ("AT", 256), ("LW", 240), ("LM", 256), ("ON", 128), ("KC", 192), ("LC", 12), ("VL", 32), ("C3", G),
          ("K6", 16), ("FT", 192), ("FR", 192), ("F2", 192), ("G2", 192), ("FE", L), ("FW", L), ("LE", 2 * L), ("YP", 12 * L), ("MN", L),
          ("MX", L), ("WN", L), ("DX", L), ("OM", L), ("HM", L), ("CH", G), ("CN", G), ("SL", 784), ("SN0", 3 * CAP), ("SN1", 3 * CAP),
          ("MB", 8), ("LR00", 3 * CAP), ("LR01", 3 * CAP), ("LR10", 3 * CAP), ("LR11", 3 * CAP)]
    f4 = [("CF", V), ("IO", 800), ("IB", 128), ("I8", 256), ("KO", 32), ("RM", 16), ("WT", 32), ("CJ", 56), ("RK", 192), ("Y8", G),
          ("KT", 192), ("KS", 192), ("KM", 16), ("NA", 32), ("THR", 16), ("TT", 16), ("DS", L), ("DC", L), ("SO", G), ("DT", 176), ("MC", 4)]
    i4 = [("CI", V), ("SI", V), ("T8", 2), ("PI", 8), ("YI", 384), ("DI", 16), ("XS", L), ("MI", 8)]
    u2 = [("CU", V), ("SU", V), ("RL", V), ("LS", 16), ("BL", 16), ("SC", 16), ("FL", 44), ("FG", 100), ("DL", 44), ("IL0", 16), ("IL1", 16),
          ("LI00", 16), ("LI01", 16), ("LI10", 16), ("LI11", 16)]
    for lst, d in ((bf, "bfloat16"), (f4, "float32"), (i4, "int32"), (u2, "uint16")):
        for nm, w in lst:
            SCRATCH[nm] = ("sbuf", [128, w], d)
    for b in range(8):
        SCRATCH["B%d" % b] = ("psum", [128, 512], "float32")


_declare()
SEMAPHORES = ["s_v", "s_s", "s_p", "s_g"] + ["d%d" % i for i in range(15)] + ["ar%d%d" % (i, b) for i in range(8) for b in range(2)] + ["lo%d" % i for i in range(8)]


def tracker(g, T):
    eng = {"v": g.vector, "s": g.scalar, "p": g.tensor, "g": g, "y": g.sync}
    known = {e: {} for e in eng}
    cnt = {e: 0 for e in eng}
    recs = {}
    total = {}

    def view(name, lo=0, hi=None, st=1, p0=0, p1=128):
        hi = SCRATCH[name][1][1] if hi is None else hi
        t = T[name]
        return (t[p0:p1, lo:hi] if st == 1 else t[p0:p1, lo:hi:st], [(name, lo, hi)])

    def ind(win, off):
        return (win[0].indirect(off[0]), win[1] + off[1])

    def need(e, rec):
        sem, val, clock, _ = rec
        if known[e].get(sem, 0) < val:
            eng[e].wait_ge(T.sem[sem], val)
            for k, x in clock.items():
                if known[e].get(k, 0) < x:
                    known[e][k] = x

    def depend(e, outs, ins):
        deps = []
        for (lst, wr) in ((ins, False), (outs, True)):
            for v in lst:
                for (name, lo, hi) in v[1]:
                    bank = SCRATCH[name][0] == "psum"
                    for (a, b, w, rec) in recs.get(name, []):
                        if bank:
                            if rec[3] != e:
                                deps.append(rec)
                        elif a < hi and lo < b and (wr or w):
                            deps.append(rec)
        deps.sort(key=lambda r: -r[1])
        for r in deps:
            need(e, r)

    def note(rec, outs, ins):
        for (lst, wr) in ((ins, False), (outs, True)):
            for v in lst:
                for (name, lo, hi) in v[1]:
                    old = recs.get(name, [])
                    if SCRATCH[name][0] == "psum":
                        recs[name] = [(0, 512, True, rec)]
                        continue
                    if wr:
                        old = [r for r in old if not (lo <= r[0] and r[1] <= hi)]
                    else:
                        old = [r for r in old if not (not r[2] and lo <= r[0] and r[1] <= hi and r[3][3] == rec[3] and rec[3] is not None)]
                    recs[name] = old + [(lo, hi, wr, rec)]

    def comp(e, fn, out, ins, *args, **kw):
        depend(e, [out], ins)
        cnt[e] += 1
        sem = "s_" + e
        rec = (sem, cnt[e], dict(known[e]), e)
        rec[2][sem] = cnt[e]
        fn(*args, **kw).then_inc(T.sem[sem], 1)
        total[sem] = cnt[e]
        note(rec, [out], ins)
        return rec

    def dma(e, sem, out, in_):
        o = [out] if len(out) > 1 else []
        i = [in_] if len(in_) > 1 else []
        depend(e, o, i)
        eng[e].dma_start(out[0], in_[0]).then_inc(T.sem[sem], 16)
        rec = (sem, 16, dict(known[e]), None)
        rec[2][sem] = 16
        total[sem] = 16
        note(rec, o, i)

    def sent(call, sem, val, srcs):
        depend("g", [], srcs)
        call()
        rec = (sem, val, dict(known["g"]), None)
        rec[2][sem] = val
        total[sem] = val
        note(rec, [], srcs)

    def arrives(sem, val, out):
        total[sem] = val
        note((sem, val, {sem: val}, None), [out], [])

    def finish():
        for k in sorted(total):
            if known["y"].get(k, 0) < total[k]:
                g.sync.wait_ge(T.sem[k], total[k])
    return view, ind, comp, dma, sent, arrives, finish, need


def rank_program(g, core, T, topo):
    rank = T.rank_of(core)
    if rank is None:
        return
    n = len(T.cores)

    def shares(c):
        q, used = T.rank_of(c), {}
        for d in sorted([T.cores[(q - 1) % n], T.cores[(q + 1) % n]], key=lambda z: len(topo.engines(c, z))):
            used[d] = [e for e in topo.engines(c, d) if not any(e in x for x in used.values())]
        return used
    nb = [(T.cores[(rank - 1) % n], 0), (T.cores[(rank + 1) % n], 1)]
    eng = shares(core)
    arrive_n = [len(shares(T.cores[(rank + 1) % n])[core]), len(shares(T.cores[(rank - 1) % n])[core])]
    local_n = sum(len(x) for x in eng.values())

    view, ind, comp, dma, sent, arrives, finish, need = tracker(g, T)
    vec, sca, ten = g.vector, g.scalar, g.tensor

    def cp(o, i): comp("v", vec.tensor_copy, o, [i], o[0], i[0])
    def tt(o, a, b, op): comp("v", vec.tensor_tensor, o, [a, b], o[0], a[0], b[0], op)
    def ts(o, a, s1, op0, s2=None, op1=None):
        ins = [a] + [s for s in (s1, s2) if isinstance(s, tuple)]
        u1 = s1[0] if isinstance(s1, tuple) else s1
        u2 = s2[0] if isinstance(s2, tuple) else s2
        if op1 is None:
            comp("v", vec.tensor_scalar, o, ins, o[0], a[0], u1, None, op0)
        else:
            comp("v", vec.tensor_scalar, o, ins, o[0], a[0], u1, u2, op0, op1)
    def ms(o, c): comp("v", vec.memset, o, [], o[0], c)
    def scan(o, a, b, init, op0, op1): comp("v", vec.tensor_tensor_scan, o, [a, b], o[0], a[0], b[0], init, op0, op1)
    def tr(o, i): comp("v", vec.transpose, o, [i], o[0], i[0])
    def red(o, i): comp("v", vec.tensor_reduce, o, [i], o[0], i[0], AxisListType.X, A.add)
    def act(o, i, f, bias=0.0): comp("s", sca.activation, o, [i], o[0], i[0], f, bias=bias)
    def mm(o, l, r, start, stop): return comp("p", ten.matmul, o, [l, r], o[0], l[0], r[0], start, stop)
    def iota(o, pat, base, cm): comp("g", g.iota, o, [], o[0], pat, base, cm, allow_small_or_imprecise_dtypes=True)
    def gfill(name, lo, hi, c): iota(view(name, lo, hi), [[0, hi - lo]], c, 0)

    I = view("IW", 16, 144)

    def zq(z, q): return view(z, 15 - q, 143 - q)

    def listed(o, z, name, lo, hi):
        for q in range(16):
            mm(o, zq(z, q), view(name, lo + q, hi, 16), q == 0, q == 15)

    def fused(src, dst, arr, lsem):
        out = []
        for d, blk in nb:
            rid, pid = topo.addr(d, core)
            out.append(RemoteDMATransfer(dst_ids=[DstId(rid=rid, pnc=pid)], dma_engine_mask=sum(1 << e for e in eng[d]),
                                         remote_sem=T.sem["%s%d" % (arr, blk)], src=src[0], dst=dst(blk)))
        sent(lambda: g.remote_dma_fused(out, local_sem=T.sem[lsem]), lsem, local_n, [src])

    dma("y", "d0", view("R", 0, V), (T.reach[:],))
    comp("g", g.iota, view("PI", 0, 1), [], T.PI[:, 0:1], [[0, 1]], 0, 1)
    iota(view("IO"), [[1, 800]], 0, 0)
    dma("s", "d1", view("P", 0, V), (T.past[:],))
    dma("y", "d2", view("CI"), (T.cand[:],))
    dma("s", "d3", view("X"), (T.x[:],))
    dma("y", "d4", view("SI"), (T.succ[:],))
    dma("s", "d5", view("T8", 0, 1, 1, 0, 8), (T.th[:],))
    fused(view("R", 0, G), lambda b: T.RF[:, V + G * b: V + G * b + G], "ar0", "lo0")
    fused(view("P", 0, G), lambda b: T.PF[:, V + G * b: V + G * b + G], "ar1", "lo1")
    for b in range(2):
        arrives("ar0%d" % b, arrive_n[b], view("RF", V + G * b, V + G * b + G))
        arrives("ar1%d" % b, arrive_n[b], view("PF", V + G * b, V + G * b + G))
    iota(view("IB"), [[16, 8], [0, 16]], 0, 0)
    for h in range(2):
        iota(view("I8", 128 * h, 128 * h + 128, 1, 0, 8), [[2, 4], [0, 32]], h, -1)

    def ko(i): return view("KO", i, i + 1)
    def pi(i): return view("PI", i, i + 1)
    def rm(i): return view("RM", i, i + 1)
    ts(pi(1), pi(0), 15, A.bitwise_and)
    ts(pi(2), pi(0), 112, A.bitwise_and)
    ts(pi(3), pi(0), 4, A.arith_shift_right, 1, A.bitwise_and)
    ts(pi(4), pi(0), 31, A.bitwise_and)
    ts(pi(5), pi(0), 1, A.bitwise_and)
    cp(ko(1), pi(2)); cp(ko(0), pi(1)); cp(ko(2), pi(3)); cp(ko(9), pi(4)); cp(ko(20), pi(5))
    ts(ko(4), pi(0), 16.0, A.add)
    ts(ko(5), ko(1), 15.0, A.add)
    ts(view("IW"), view("IO", 0, 160), ko(4), A.is_equal)
    ts(view("Z1"), view("IO", 0, 144), ko(5), A.is_equal)
    ts(view("KC"), view("IO", 0, 192), 0.0, A.mult, ko(0), A.add)
    ts(view("NI"), I, -1.0, A.mult)
    ts(view("ZO"), view("Z1"), WO, A.mult)
    ts(view("KC"), view("KC"), 1.0 / 16, A.mult)
    gfill("XF", V, W, int(BIGX))
    gfill("UT", 0, 800, 0)
    for nm, w in (("RK", 192), ("FT", 192), ("F2", 192), ("WT", 16)):
        gfill(nm, 0, w, 0)
    for i in range(10):
        gfill("WT", i, i + 1, 2 ** i)
    gfill("BF", V, W + L, 0)
    gfill("R", V, 784, 0); gfill("P", V, 784, 0)
    gfill("LW", 0, 240, 0); gfill("LM", 0, 256, 0)
    gfill("RF", W, W + L, 0)
    gfill("RST", 0, NR, 0)
    gfill("C3", 0, G, 113)
    for nm in ("GB", "GR", "GP"):
        for b in range(2):
            gfill(nm, GB_ * b + G, GB_ * b + GB_, 0)

    def spread(dst, src, t):
        return [lambda k=k: cp(view(dst, k, NE, 16), view(src, t, V, 4)) for k in range(16)]

    def spread_s(dst, src, t):
        act(view(dst), ind(view(src, 0, V), view("RL", L * t, L * t + L)), AF.Copy)

    def run(l):
        for f in l:
            f()

    def xmask(dst, t):
        ts(view(dst, t, V, 4), view("X", t, V, 4), 0.0, A.mult, BIGX, A.add)
    for r in range(2):
        ts(view("RL", L * r, L * r + L), view("IO", 0, V, 4), float(r), A.add)
    cp(view("RF", 0, V), view("R", 0, V))
    run(spread("RVB0", "R", 0))
    cp(view("PF", 0, V), view("P", 0, V))
    cp(view("CU", 0, L), view("CI", 0, V, 4))
    cp(view("XF", 0, V), view("X"))
    xmask("XF", 0)
    spread_s("XVB", "X", 0)
    run(spread("PVB0", "P", 0))

    def key_x_gather(t):
        act(view("GX"), ind(view("XF"), view("CU", L * t, L * t + L)), AF.Copy)

    def key_start():
        mm(view("B0", 0, 192), I, view("KC"), True, False)

    CH = [(c, min(c + 512, NE), "B%d" % (2 + c // 512)) for c in range(0, NE, 512)]

    def x_diff(lo, hi):
        for c, e, b in CH[lo:hi]:
            mm(view(b, 0, e - c), I, view("GX", c, e), True, False)
            mm(view(b, 0, e - c), view("NI"), view("XVB", c, e), False, True)

    def x_size(lo, hi):
        for c, e, b in CH[lo:hi]:
            act(view("AX", c, e), view(b, 0, e - c), AF.Abs)

    def key_add(z, src, lo, hi, stop=False):
        for k in range(16):
            mm(view("B0", lo, hi), zq(z, k), view(src, 16 * lo + k, 16 * hi, 16), False, stop and k == 15)

    def sig_part(which, first, last, bank=2):
        z = {"P": "BO", "R": "BN", "BF": "BW"}[which]
        for h in range(2):
            mm(view("B%d" % (bank + h), 0, 336), view(z), view(which, 336 * h, 336 * h + 336), first, last)

    def key_bits(t):
        act(view("BC"), ind(view("BF", 0, W), view("CU", L * t, L * t + L)), AF.Copy)
    ts(view("BO"), view("IB"), ko(1), A.is_equal)
    ts(view("BN"), view("BO"), -1.0, A.mult)
    sig_part("P", True, False, 6); sig_part("R", False, True, 6)
    key_x_gather(0)
    for h in range(2):
        act(view("SO", 336 * h, 336 * h + 336), view("B%d" % (6 + h), 0, 336), AF.Copy)
    key_start()
    ts(view("E8", 0, 256, 1, 0, 8), view("I8", 0, 256, 1, 0, 8), 0.0, A.is_equal)
    ts(view("MI", 4, 5, 1, 0, 8), view("T8", 0, 1, 1, 0, 8), 4080, A.bitwise_and)
    ts(view("MI", 5, 6, 1, 0, 8), view("T8", 0, 1, 1, 0, 8), 15, A.bitwise_and)
    cp(view("MB", 4, 6, 1, 0, 8), view("MI", 4, 6, 1, 0, 8))
    for h in range(2):
        for i in range(2):
            mm(view("B1", h, h + 1), view("E8", 128 * h, 128 * h + 128, 1, 0, 8), view("MB", 4 + i, 5 + i, 1, 0, 8), i == 0, i == 1)

    def chain_constants():
        for b in range(6):
            cp(view("THR", 2 * b, 2 * b + 2), view("B1", 0, 2))
        cp(view("YI", 0, 50), view("IO", 0, 50))
        for i in range(5):
            ts(view("YI", 64 + i, 65 + i), pi(0), i, A.arith_shift_right, 1, A.bitwise_and)
        for i in range(5):
            ts(view("YI", 80 + 50 * i, 130 + 50 * i), view("YI", 0, 50), i + 1, A.arith_shift_right, 1, A.bitwise_and)
        ts(view("KO", 24, 29), view("YI", 64, 69), 2.0, A.mult, -1.0, A.add)
        for i in range(5):
            ts(view("UT", 5 + i, 800, 16), view("YI", 80 + 50 * i, 130 + 50 * i), 2.0, A.mult, -1.0, A.add)
        for i in range(5):
            ts(view("UT", i, 800, 16), view("IO", 0, 50), 0.0, A.mult, ko(24 + i), A.add)
        tr(view("BT"), view("UT"))
        cp(view("BF", 0, V), view("BT", 0, V))
        key_bits(0)
        spread_s("PVB1", "P", 1)
        ts(view("RK", 0, 192, 16), view("IO", 0, 12), 0.0, A.mult, 2.0 ** 28, A.add)
        for h in range(2):
            ts(view("FT", 16 * h + 12, 192, 32), view("IO", 0, 192, 32), ko(9), A.add)
        for i in (13, 14, 15):
            ts(view("FT", i, 192, 16), view("IO", 0, 12), 0.0, A.mult, 1.0, A.add)
        for w in range(2):
            ts(view("LC", 6 * w, 6 * w + 6), view("IO", 16 * w, 192, 32), ko(0), A.add, 16.0, A.mult)
        ts(ko(3), ko(2), -1.0, A.mult, 1.0, A.add)
        ts(view("RM"), view("IO", 0, 16), ko(0), A.is_equal)
        for h in range(2):
            for w in range(2):
                z = 16 - 16 * (h - w)
                ts(view("SW", 128 * (2 * h + w), 128 * (2 * h + w) + 128), view("IW", z, z + 128), ko(2 if w else 3), A.mult, 16.0, A.mult)
        ts(ko(6), ko(0), 10.0, A.is_lt)
        ts(ko(16), rm(13), 256.0, A.mult)
        tt(ko(17), rm(10), rm(11), A.add)
        ts(ko(15), ko(6), WB, A.mult)
        ts(ko(17), ko(17), -256.0, A.mult)
        ts(view("AT", 0, 128), I, ko(15), A.mult)
        tt(ko(17), ko(17), rm(12), A.subtract)
        for d, c in ((-3, ko(16)), (-2, ko(16)), (-1, rm(13)), (3, ko(17))):
            ts(view("AT", 128, 256), view("IW", 16 - d, 144 - d), c, A.mult)
            tt(view("AT", 0, 128), view("AT", 0, 128), view("AT", 128, 256), A.add)
        for h in range(2):
            ts(view("AE", 128 * h, 128 * h + 128), view("AT", 0, 128), ko(2 if h else 3), A.mult)
        tt(view("WT", 16, 32), view("WT", 0, 16), view("RM"), A.mult)
        red(ko(10), view("WT", 16, 32))
        ts(ko(7), ko(10), 0.5, A.mult)
        ts(view("ZB"), view("Z1"), ko(7), A.mult)

    def rival_constants():
        ts(view("BQ"), view("BO"), rm(0), A.mult, 512.0, A.mult)
        ms(view("LW", 112, 128), 512.0)
        ts(ko(18), ko(4), 75.0, A.is_lt, 512.0, A.mult)
        ts(ko(19), ko(18), -1.0, A.mult, 512.0, A.add)
        ts(view("LM", 112, 128), view("LM", 112, 128), ko(18), A.add)
        ts(view("LM", 128, 144), view("LM", 128, 144), ko(19), A.add)
        ts(view("TT", 0, 12), view("THR", 0, 12), 4096.0, A.min)

    def merge_constants():
        ts(ko(13), rm(13), -1536.0, A.mult)
        ts(ko(14), rm(14), -0.5, A.mult)
        tt(ko(13), ko(13), rm(12), A.subtract)
        tt(ko(14), ko(14), ko(7), A.add)
        ts(view("FL"), view("IO", 0, V, 16), ko(0), A.add)
        tt(ko(13), ko(13), ko(14), A.add)
        ts(view("VL", 0, 11), view("IO", 0, L, 16), ko(0), A.add)
        ts(view("ZS"), view("Z1"), ko(13), A.mult)
        ms(view("VL", 16, 27), float(DUMP))
        cp(view("SU", 2 * L, 3 * L), view("SI", 2, V, 4))
        cp(view("CF"), view("CI"))
        cp(view("XM"), view("X"))
        ts(view("RST", 0, NR, 16), view("IO", 0, NR // 16), 0.0, A.mult, 512.0, A.add)

    def exchange_constants():
        ts(view("BW"), view("BO"), ko(7), A.mult, 8192.0, A.mult)
        ts(view("Y8"), view("IO", 0, G), 8192.0, A.mult, -511.5 * 8192.0, A.add)
        tt(view("SO"), view("SO"), view("Y8"), A.add)
        cp(view("CU", L, 2 * L), view("CI", 1, V, 4))
        ts(view("Z0"), view("Z1"), rm(0), A.mult)
        ts(view("ZN"), view("Z0"), -1024.0, A.mult)
        ts(view("CJ", 0, 42), view("IO", 0, G, 16), ko(0), A.add, 112.0 - 1023.0, A.add)
        ts(view("CJ", 44, 51), view("IO", 0, CAP, 16), ko(0), A.add, 672.0, A.add)
        ms(view("ON"), 1.0 / 16)
        ts(view("RL", 2 * L, 3 * L), view("IO", 0, V, 4), 2.0, A.add)

    def ghost_constants():
        for b in range(2):
            w = GB_ * b
            for i, (nm, src) in enumerate((("GR", view("RF", V + G * b, V + G * b + G)), ("GP", view("PF", V + G * b, V + G * b + G)), ("GB", view("BT", 0, G)))):
                dma("y", "d%d" % (9 + 3 * b + i), view(nm, w, w + G), src)

    def list_constants(t):
        out = [lambda: cp(view("CU", L * t + L, L * t + 2 * L), view("CI", t + 1, V, 4))]
        if t == 1:
            out.append(lambda: cp(view("SU", 3 * L, 4 * L), view("SI", 3, V, 4)))
            out.append(lambda: ts(view("RL", 3 * L, 4 * L), view("IO", 0, V, 4), 3.0, A.add))
        return out

    later = []

    def fill(k):
        for _ in range(min(k, len(later))):
            later.pop(0)()

    for t in range(RO):
        last = t == RO - 1
        cu = lambda lo, hi: view("CU", L * t + lo, L * t + hi)
        su = lambda r, lo, hi: view("SU", L * r + lo, L * r + hi)
        actv = lambda nm: view(nm, t, V, 4)
        bl = view("BL", 0, 11)
        pvb, rvb = "PVB%d" % (t % 2), "RVB%d" % (t % 2)
        for lo, hi in ((0, 112), (112, L)):
            tt(view("A1", 16 * lo, 16 * hi), ind(view("RF", 0, W), cu(lo, hi)), view(pvb, 16 * lo, 16 * hi), A.is_le)
        for lo, hi in ((0, 112), (112, L)):
            tt(view("A2", 16 * lo, 16 * hi), ind(view("PF"), cu(lo, hi)), view(rvb, 16 * lo, 16 * hi), A.is_ge)
        if 0 < t < RO - 1:
            spread_s("PVB%d" % ((t + 1) % 2), "P", t + 1)
            spread_s("RVB%d" % ((t + 1) % 2), "R", t + 1)
        key_add("ZO", "A1", 0, 112)
        if t:
            key_add("Z1", "AX", 32 * XC, L)
        key_add("ZO", "A1", 112, L)
        if t == 0:
            x_diff(0, 6)
            x_size(0, 6)
            key_add("Z1", "AX", 0, L)
        key_add("ZO", "A2", 0, 112)
        key_add("ZO", "A2", 112, L, True)
        if t == 0:
            chain_constants()
            ghost_constants()
        if not last:
            later.extend(list_constants(t) if t else [])
            later.extend(spread("XVB", "X", t + 1))
        fill(8)
        tr(view("KT"), view("B0", 0, 192))
        scan(view("KS"), view("RK"), view("KT"), 0.0, A.add, A.min)
        ts(view("KM", 0, 12), view("KS", 15, 192, 16), 16000.0, A.min)
        ts(view("DI", 0, 12), view("KM", 0, 12), -0.47, A.add)
        tt(view("K6", 0, 12), view("KM", 0, 12), view("DI", 0, 12), A.subtract)
        mm(view("B1", 0, 12), I, view("LC"), True, False)
        for w in range(2):
            for h in range(2):
                j = 128 * (2 * h + w)
                mm(view("B1", 6 * w, 6 * w + 6), view("SW", j, j + 128), view("K6", h, 12, 2), False, w == 1 and h == 1)
        cp(view("FT", 10, 192, 16), view("DI", 0, 12))
        tt(view("FT", 11, 192, 16), view("DI", 0, 12), view("FT", 10, 192, 16), A.subtract)
        ts(view("OM"), view("B0", 0, L), WO, A.is_ge)
        tr(view("FR"), view("FT"))
        for w in range(2):
            cp(view("LS", w, 12, 2), view("B1", 6 * w, 6 * w + 6))
        tt(view("FE"), ind(view("BC"), view("LS", 0, 11)), view("FR", 0, L), A.add)
        mm(view("B6", 0, L), view("AE", 0, 128), view("FE"), True, True)
        mm(view("B7", 0, L), view("AE", 128, 256), view("FE"), True, True)
        cp(view("LE", 0, L), view("B6", 0, L))
        act(view("LE", L, 2 * L), view("B7", 0, L), AF.Copy)
        listed(view("B0", 0, 11), "ZB", "FE", 0, L)
        if t == 0:
            rival_constants()
        tt(view("NA", 0, 12), view("KM", 0, 12), view("TT", 0, 12), A.is_ge)
        ts(view("NA", 16, 28), view("KM", 0, 12), 4096.0, A.is_ge, 2.0, A.mult)
        cp(view("DS"), actv("SI"))
        tt(view("F2", 0, 192, 16), view("NA", 0, 12), view("NA", 16, 28), A.add)
        tr(view("G2"), view("F2"))
        fill(4)
        done = {}
        for i in (0, 1, 2, 3, 4, 5, 6, 7, 8, 10, 9, 11):
            a, j = TILES[i]
            c = (0, 117, 234)[j]
            if i in (9, 11):
                need("p", done[i - 1])
            done[i] = mm(view("B%d" % (2 + i // 2), L * (i % 2), L * (i % 2) + L, 1, 0, 118), view("LE", c, c + 118, 1, 32 * a, 32 * a + 32),
                         view("FE", 0, L, 1, 32 * a, 32 * a + 32), True, True)
        ts(bl, view("B0", 0, 11), 511.5, A.add)
        mm(view("B0", 64, 64 + L), view("BQ"), view("G2", 0, L), True, True)
        tt(view("MN"), ind(view("R"), bl), view(rvb, 0, NE, 16), A.min)
        mm(view("B1", 0, L), I, view("MN"), True, False)
        mm(view("B1", 0, L), view("BQ"), view("G2", 0, L), False, False)
        for b in range(6):
            o = view("YP", 352 * b, 352 * b + 352, 1, 0, 118)
            i = view("B%d" % (2 + b), 0, 352, 1, 0, 118)
            if b % 2 == 1:
                ts(o, i, 10 * WB, A.is_gt)
            else:
                act(o, i, AF.Relu, -10 * WB)
            for i in (2 * b, 2 * b + 1):
                a, j = TILES[i]
                if j == 1:
                    l = view("LM", 112 - 32 * a, 240 - 32 * a, 1, 0, 118)
                else:
                    k = 112 - 16 * (2 * a + j // 2)
                    l = view("LW", k, k + 128, 1, 0, 118)
                mm(view("B1", 0, L), l, view("YP", L * i, L * i + L, 1, 0, 118), False, i == 11)
        if t == 0:
            merge_constants()
        ts(view("HM"), view("B0", 64, 64 + L), 1000.0, A.is_lt)
        tt(view("DS"), ind(view("SI"), bl), view("DS"), A.subtract)
        ts(view("DS"), view("DS"), ko(20), A.mult)
        tt(view("MX"), ind(view("P"), bl), view(pvb, 0, NE, 16), A.max)
        fill(10)

        def candidates():
            cp(view("DC"), actv("CF"))
            tt(view("HM"), view("HM"), view("OM"), A.mult)
            tt(view("DC"), ind(view("CF"), bl), view("DC"), A.subtract)
            tt(view("DC"), view("DC"), view("HM"), A.mult)
            tt(actv("CF"), actv("CF"), view("DC"), A.add)

        def halves():
            tt(view("XS"), ind(view("XM"), bl), actv("X"), A.add)
            ts(view("XS"), view("XS"), 1, A.arith_shift_right)
            tt(view("DX"), view("XS"), actv("X"), A.subtract)

        def features():
            tt(view("DX"), view("DX"), view("WN"), A.mult)
            tt(actv("X"), actv("X"), view("DX"), A.add)
        mm(view("B0", 0, 11), I, view("VL", 0, 11), True, False)
        mm(view("B0", 0, 11), I, view("VL", 16, 27), False, False)
        ts(view("WN"), view("B1", 0, L), 512.0, A.is_lt)
        tt(view("FW"), view("FE"), view("WN"), A.mult)
        tt(actv("R"), view("B1", 0, L), actv("R"), A.min)
        act(view("RF", 0, V), ind(view("R", 0, V), view("FL")), AF.Copy)
        for q in range(16):
            mm(view("B0", 0, 11), zq("ZS", q), view("FW", q, L, 16), False, q == 15)
        tt(view("DS"), view("DS"), view("WN"), A.mult)
        tt(actv("SI"), actv("SI"), view("DS"), A.add)
        cp(view("SC", 0, 11), view("B0", 0, 11))
        cp(su(t, 0, L), actv("SI"))
        cp(ind(view("RF"), view("SC", 0, 11)), actv("R"))
        o = (t + 2) % 4
        rf = view("RF", 0, W)
        v3 = VL3 if last else V3
        for lo, hi in ((0, 88), (88, L)):
            act(view("GA", 16 * lo, 16 * hi), ind(rf, su(o, lo, hi)), AF.Copy)
        for lo, hi in ((v3, 112), (112, L)):
            act(view("GA", NE + 16 * lo, NE + 16 * hi), ind(rf, su(t, lo, hi)), AF.Copy)
        cp(view("GA", NE, NE + 16 * v3), ind(rf, su(t, 0, v3)))

        def low(r, lo, hi):
            a, e = (NE if r == t else 0) + 16 * lo, (NE if r == t else 0) + 16 * hi
            scan(view("GS", a, e), view("RST", 0, e - a), view("GA", a, e), 0.0, A.add, A.min)
            z = view("R", r + 4 * lo, r + 4 * hi - 3, 4)
            tt(z, view("GS", a + 15, e, 16), z, A.min)
        if not last:
            cp(ind(view("BF"), view("SC", 0, 11)), view("BT", t, V, 4))
            listed(view("B0", 0, 44), "ZB", "BF", 0, V)
            tt(view("MX"), view("MX"), view("WN"), A.mult)
            tt(actv("P"), actv("P"), view("MX"), A.max)
            if t == 0:
                exchange_constants()
            sig_part("P", True, False)
            sig_part("BF", False, False)
        low(t, 0, v3)
        if last:
            halves()
            features()
            dma("y", "d7", (T.yx[:],), view("X"))
        low(o, 0, 88)
        if last:
            candidates()
            dma("y", "d8", (T.yc[:],), view("CF"))
        else:
            ts(view("FL"), view("B0", 0, 44), 511.5, A.add)
        low(o, 88, L)
        if not last:
            halves()
        low(t, v3, 112)
        low(t, 112, L)
        if last:
            dma("y", "d6", (T.yr[:],), view("R", 0, V))
            break
        sig_part("R", False, True)
        for h in range(2):
            tt(view("CH", 336 * h, 336 * h + 336), view("B%d" % (2 + h), 0, 336), view("SO", 336 * h, 336 * h + 336), A.not_equal)
        for h in range(2):
            act(view("SO", 336 * h, 336 * h + 336), view("B%d" % (2 + h), 0, 336), AF.Copy)
        act(view("PF", 0, V), ind(view("P", 0, V), view("FL")), AF.Copy)
        for q in range(16):
            mm(view("B1", 0, 42), zq("ZN", q), view("CH", q, G, 16), q == 0, False)
        scan(view("CN"), view("CH"), view("C3"), 0.0, A.add, A.min)
        for q in range(16):
            mm(view("B1", 0, 42), zq("Z0", q), view("CN", q, G, 16), False, q == 15)
        features()
        cp(actv("XM"), actv("X"))
        xmask("XM", t + 1)
        act(view("XF", 0, V), ind(view("XM"), view("FL")), AF.Copy)
        key_x_gather(t + 1)
        key_bits(t + 1)
        cp(view("SL", 0, CAP), view("BT", G, G + CAP))
        ts(view("DT", 0, 42), view("B1", 0, 42), -911.0, A.is_ge, 4096.0, A.mult)
        tt(view("DT", 44, 86), view("B1", 0, 42), view("DT", 0, 42), A.add)
        tt(view("DT", 88, 130), view("DT", 44, 86), view("CJ", 0, 42), A.min)
        ts(view("DL", 0, 42), view("DT", 88, 130), 1023.0, A.add)
        cp(ind(view("SL"), view("DL", 0, 42)), view("BT", 0, G))
        e = t % 2
        il, sn = "IL%d" % e, "SN%d" % e
        jl = view(il, 0, 7)
        listed(view("B1", 0, 7), "ZB", "SL", 0, CAP)
        ms(view(il, 7, 8), 0); ms(view(il, 15, 16), 0)
        fill(2)
        ts(jl, view("B1", 0, 7), 511.5, A.add)
        cp(view(sn, 2 * CAP, 3 * CAP), ind(view("BF"), jl))
        ts(view("DT", 132, 139), view("B1", 0, 7), 511.5, A.add)
        listed(view("B1", 0, 7), "ZB", sn, 2 * CAP, 3 * CAP)
        cp(view(sn, 0, CAP), ind(view("R"), jl))
        cp(view(sn, CAP, 2 * CAP), ind(view("P"), jl))
        fused(view(sn), lambda b: T["LR%d%d" % (e, b)][:], "ar%d" % (2 + 2 * t), "lo%d" % (2 + 2 * t))
        tt(view("DT", 140, 147), view("CJ", 44, 51), view("DT", 132, 139), A.subtract)
        ts(view("DT", 148, 155), view("B1", 0, 7), 160.0, A.is_ge)
        tt(view("DT", 148, 155), view("DT", 148, 155), view("DT", 140, 147), A.mult)
        tt(view("DT", 148, 155), view("DT", 148, 155), view("DT", 132, 139), A.add)
        cp(view(il, 8, 15), view("DT", 148, 155))
        fused(view(il), lambda b: T["LI%d%d" % (e, b)][:], "ar%d" % (3 + 2 * t), "lo%d" % (3 + 2 * t))
        for b in range(2):
            arrives("ar%d%d" % (2 + 2 * t, b), arrive_n[b], view("LR%d%d" % (e, b)))
            arrives("ar%d%d" % (3 + 2 * t, b), arrive_n[b], view("LI%d%d" % (e, b)))
        red(view("MC", 0, 1), view("WN"))
        cp(view("MB", 0, 1), view("MC", 0, 1))
        mm(view("B1", 0, 1), view("ON"), view("MB", 0, 1), True, True)
        cp(view("RF", 0, V), ind(view("R", 0, V), view("FL")))
        fill(99)
        if t == 0:
            spread_s("RVB1", "R", 1)
        key_start()
        x_diff(0, XC)
        x_size(0, XC)
        cp(view("MI", 0, 1), view("B1", 0, 1))
        candidates()
        ts(view("MI", 1, 2), view("MI", 0, 1), 31, A.bitwise_and)
        cp(view("MC", 1, 2), view("MI", 1, 2))
        ts(view("TT", 0, 12), view("THR", 0, 12), view("MC", 1, 2), A.add, 4096.0, A.min)

        def taken(nm, lo, c):
            for b in range(2):
                cp(ind(view(nm, GB_ * b, GB_ * b + GB_), view("LI%d%d" % (e, b), lo, lo + 7)), view("LR%d%d" % (e, b), c, c + CAP))

        def renamed(dst, nm, b):
            return view(dst, V + G * b, V + G * b + G), ind(view(nm, GB_ * b, GB_ * b + GB_), view("FG", 50 * b, 50 * b + 42))
        taken("GB", 8, 2 * CAP)
        for q in range(16):
            mm(view("B1", 0, 92), zq("ZB", q), view("GB", q, 1472, 16), q == 0, q == 15)
        x_diff(XC, 6)
        key_add("Z1", "AX", 0, 32 * XC)
        taken("GR", 0, 0)
        taken("GP", 0, CAP)
        ts(view("FG", 0, 92), view("B1", 0, 92), 511.5, A.add)
        cp(*renamed("RF", "GR", 0))
        if t:
            act(*renamed("RF", "GR", 1), AF.Copy)
        else:
            cp(*renamed("RF", "GR", 1))
        for b in range(2):
            act(*renamed("PF", "GP", b), AF.Copy)
        x_size(XC, 6)
    finish()
